import numpy as np, ml_dtypes
CORES = [25,29,65,69,153,157,193,197]
N = 8
import mx_ref
BF = ml_dtypes.bfloat16
def cols(t, e):
    v = np.concatenate([t.reshape(128, -1, 4), np.zeros((128, 1, 4), BF)], axis=1)
    return np.ascontiguousarray(v[:, e]).reshape(128, -1)
def cut(t, i, w=512):
    return t[:, w * i:w * i + w]
def tile(rs):
    return np.stack(rs, axis=2).reshape(128, -1).astype(BF)
def pick(q, e):
    c = np.concatenate([q[0].reshape(128, -1, 4), np.zeros((128, 1, 4), np.uint8)], axis=1); s = np.concatenate([q[1], np.ones((16, 1), np.uint8)], axis=1)
    return (np.ascontiguousarray(c[:, e].reshape(128, -1)), np.ascontiguousarray(s[:, e]))
def join(*qs):
    return (np.concatenate([q[0] for q in qs], axis=1), np.concatenate([q[1] for q in qs], axis=1))
def put(q, e, v):
    c, s = q[0].reshape(128, -1, 4).copy(), q[1].copy(); c[:, e] = v[0].reshape(128, -1, 4); s[:, e] = v[1]
    return (c.reshape(128, -1), s)
def pk(c, s):
    return (np.ascontiguousarray(c), mx_ref.live(s))
def emit(q):
    return q[0], q[1]
def decode(q):
    o = []
    for b in range(4):
        e = np.zeros((128, 128, 4), np.float32); e[np.arange(128), np.arange(128), b] = 1
        o.append(mx_ref.matmul(mx_ref.quantize(e.reshape(128, 512).astype(BF)), q))
    return np.stack(o, axis=2).reshape(128, -1)
def f(rng, *shape):
    return mx_ref.flush((rng.standard_normal(shape, dtype=np.float32) * np.exp2(rng.integers(-2, 3, shape[:-1] + (1,)))).astype(BF))
def wide(rng, *shape, cols=0):
    v = rng.standard_normal(shape, dtype=np.float32) * np.exp2(rng.integers(-12, 13, shape)).astype(np.float32)
    if cols: v *= np.repeat(np.exp2(rng.integers(-cols, cols + 1, shape[:-2] + (1, shape[-1] // 4))) * (rng.random(shape[:-2] + (1, shape[-1] // 4)) > 0.0625), 4, axis=-1).astype(np.float32)
    return mx_ref.flush(v.astype(BF))
T, CAPP, CAPR = 128, 48, 16
def big(v, k):
    v = v.astype(np.float32) * np.float32(k)
    v[np.abs(v) < np.float32(2.0 ** -6)] = 0
    return v.astype(BF)
def same(t):
    return np.repeat(t[None], N, axis=0)
def only(t, k):
    t = np.array(t)
    t[:, 4 * k:] = 0
    return t
def plain(rng):
    return {"x": f(rng, N, 128, 4 * T), "gr": big(f(rng, N, 128, 4 * T), 8), "rt": same(only(f(rng, 128, 512), N)), "w": f(rng, N, 128, 2048), "ub": big(f(rng, N, 128, 2048), 4), "pr": same(only(f(rng, 128, 512), 1)), "v": f(rng, N, 128, 512)}
def deal(rng, n, among):
    m, j, p = len(among), np.arange(n), rng.permutation(among)
    return np.stack([p[j % m], p[(j + 1 + j // m % (m - 1)) % m]], axis=1)
def routed(rng, to, far=False):
    g = np.arange(128) // (128 // N)
    rt = np.zeros((128, 128, 4), np.float32)
    rt[np.arange(128), g, 0] = 1 + rng.random(128)
    x = rng.standard_normal((N, 128, T, 4)) * (2 if far else 8)
    low = 0.125 * rng.choice([-1.0, 1.0], (N, 128, T))
    first, second = to[:, None, :, 0] == g[None, :, None], to[:, None, :, 1] == g[None, :, None]
    size = np.where(first, low, np.where(second, -4.0, -16.0)) if far else np.where(first, 16.0, np.where(second, 2.0, low))
    x[..., 0] = size * (1 + rng.random((N, 128, T)))
    if far: x, rt = x * 2.0 ** 25, rt * np.float32(2.0 ** 29)
    return {"x": mx_ref.flush(x.reshape(N, 128, 4 * T).astype(np.float32).astype(BF)), "rt": same(rt.reshape(128, 512).astype(BF))}
def setup_inputs(rng):
    return plain(rng)
def setup_inputs_crowd(rng):
    h = int(rng.integers(0, N))
    rest, n, to = np.delete(np.arange(N), h), [CAPP, T, CAPP + 1, CAPR, 0, CAPR + 1, CAPR - 1, 1], np.zeros((N, T, 2), int)
    for i in range(N):
        t = deal(rng, T, rest)
        t[np.arange(n[i]), rng.integers(0, 2, n[i])] = h
        to[(h + 1 + i) % N] = t[rng.permutation(T)]
    d = {**plain(rng), **routed(rng, to)}
    sign, pr = rng.choice([-1.0, 1.0], (128, 1, 4)), np.zeros((128, 128, 4), np.float32)
    pr[:, :1] = 2.0 ** 29 * sign * (1 + rng.random((128, 1, 4)))
    gr = 2.0 ** 28 * sign[None] * (1 + rng.random((N, 128, T, 4))) * rng.choice([-1.0, 1.0], (N, 1, T, 1))
    d["pr"] = same(pr.reshape(128, 512).astype(BF))
    d["gr"] = gr.reshape(N, 128, 4 * T).astype(np.float32).astype(BF)
    d["ub"] = (d["ub"].astype(np.float32) * np.float32(2.0 ** -22)).astype(BF)
    return d
def setup_inputs_dead(rng):
    rest = np.delete(np.arange(N), int(rng.integers(0, N)))
    to, dead = np.zeros((N, T, 2), int), np.zeros((N, T), bool)
    for q in range(N):
        s = rng.permutation(T)
        to[q] = deal(rng, T, rest)[s]
        dead[q] = s // (N - 1) % 4 != 0
    d = {**plain(rng), **routed(rng, to)}
    x = d["x"].astype(np.float32).reshape(N, 128, T, 4)
    x[..., 1:] = 16 * (1 + rng.random((N, 128, T, 3))) * np.where(dead, 1.0, -1.0)[:, None, :, None]
    d["x"] = x.reshape(N, 128, 4 * T).astype(BF)
    w = np.array(d["w"])
    w[rng.permutation(rest)[:N // 2]] = (-1 - rng.random((N // 2, 128, 2048))).astype(np.float32).astype(BF)
    d["w"] = w
    return d
def setup_inputs_one(rng):
    h = int(rng.integers(0, N))
    to = np.full((N, T, 2), h)
    for q in range(N): to[q, :, 1] = rng.permutation(deal(rng, T, np.delete(np.arange(N), h))[:, 0])
    return {**plain(rng), **routed(rng, to, far=True)}
def setup_inputs_spread(rng):
    d = plain(rng)
    x = (wide(rng, N, 128, 4 * T, cols=6).astype(np.float32) * np.float32(2.0 ** 8)).reshape(N, 128, T, 4)
    for q in range(N):
        i = rng.permutation(T)[:T // 8]
        x[q][:, i] = 2.0 ** -29 * (1 + rng.random((128, i.size, 4))) * rng.choice([-1.0, 1.0], (128, i.size, 4))
    d["x"] = x.reshape(N, 128, 4 * T).astype(BF)
    d["rt"] = (d["rt"].astype(np.float32) * np.float32(2.0 ** 20)).astype(BF)
    d["gr"] = big(wide(rng, N, 128, 4 * T, cols=3), 16)
    return d
def setup_inputs_ties(rng):
    u, o = sorted(rng.permutation(N)[:2].tolist())
    rest = np.delete(np.arange(N), [u, o])
    to, at = np.zeros((N, T, 2), int), []
    for q in range(N):
        t, s = deal(rng, T, rest), rng.permutation(T)
        t[:T // 2] = np.array([u, rest[0]])
        t[T // 2:T // 2 + 4, 1] = u
        to[q] = t[s]
        at.append(np.flatnonzero(s < T // 2))
    d = {**plain(rng), **routed(rng, to)}
    r = np.array(d["rt"]).reshape(N, 128, 128, 4)
    r[:, :, o] = r[:, :, u]
    x, g = d["x"].astype(np.float32).reshape(N, 128, T, 4), d["gr"].astype(np.float32).reshape(N, 128, T, 4)
    for q in range(N):
        i = at[q]
        x[q][:, i] = x[q][:, i[:1]].copy()
        g[q][:, i] = g[q][:, i[:1]].copy() * rng.choice([-1.0, 1.0], i.size)[None, :, None]
    return {**d, "x": x.reshape(N, 128, 4 * T).astype(BF), "gr": g.reshape(N, 128, 4 * T).astype(BF), "rt": r.reshape(N, 128, 512)}
def check_inputs(d):
    b = []
    for k in ("x", "gr", "rt", "w", "ub", "pr", "v"):
        a = np.abs(d[k].astype(np.float32))
        if not (np.isfinite(a).all() and ((a == 0) | (a >= 2.0 ** -30) & (a <= 2.0 ** 30)).all()): b.append("a value of " + k)
    for k, n in (("rt", N), ("pr", 1)):
        a = d[k].astype(np.float32)
        if (a != a[:1]).any(): b.append(k + " differs between ranks")
        if (a[:, :, 4 * n:] != 0).any(): b.append(k + " has numbers behind its first columns")
    return b
def reference(x, gr, rt, w, ub, pr, v):
    qz = lambda t: mx_ref.quantize(np.ascontiguousarray(t))
    to = []
    for q in range(N):
        s = mx_ref.matmul(qz(rt[q]), qz(x[q]))[:N] + np.float32(0)
        to.append(np.argsort(-s, axis=0, kind="stable")[:2])
    everyx, everyg = np.concatenate([x[q] for q in range(N)], axis=1), np.concatenate([gr[q] for q in range(N)], axis=1)
    came = np.zeros((N, 128, 2 * T, 4), np.float32)
    ct = np.zeros((N, 1, T), np.float32)
    for e in range(N):
        taken = [np.flatnonzero((to[q] == e).any(axis=0))[:CAPP] for q in range(N)]
        at = np.full((N, CAPP), -1)
        for q in range(N): at[q, :taken[q].size] = T * q + taken[q]
        at = at.reshape(-1)
        xs, gs = qz(cols(everyx, at)), qz(cols(everyg, at))
        forward = np.stack([mx_ref.matmul(qz(cut(w[e], i)), xs) for i in range(4)], axis=2).reshape(128, -1)
        m = qz(np.where(forward > 0, decode(gs), np.float32(0)).astype(BF))
        strength = np.abs(mx_ref.matmul(qz(pr[e]), m)[0])
        dx = decode(qz(tile([mx_ref.matmul(qz(cut(ub[e], i)), m) * np.float32(0.0625) for i in range(4)]))).reshape(128, -1, 4)
        for q in range(N):
            k = np.argsort(-strength[CAPP * q:CAPP * q + taken[q].size], kind="stable")[:CAPR]
            j = taken[q][k]
            second = (to[q][1, j] == e).astype(int)
            came[q][:, T * second + j] = dx[:, CAPP * q + k]
            ct[q, 0, j] += 1 + second
    oc, osc, y = np.zeros((N, 128, 4 * T), np.uint8), np.zeros((N, 16, T), np.uint8), np.zeros((N, 128, T), np.float32)
    for q in range(N):
        z = qz((came[q][:, :T] + came[q][:, T:]).reshape(128, 4 * T).astype(BF))
        oc[q], osc[q] = emit(z)
        y[q] = mx_ref.matmul(qz(v[q]), z)
    return {"oc": oc, "osc": osc, "ct": ct, "y": y}

@@ -1,0 +1,524 @@
+from concourse.bass import DstId, RemoteDMATransfer
+from concourse.mybir import dt, AluOpType, AxisListType, ActivationFunctionType
+
+OP, AF = AluOpType, ActivationFunctionType
+N, CAPP, CAPR = 8, 48, 16
+SIM = 256
+BIG = 9.0e29
+NS = 7
+NV = 16 - NS
+OWN = 130
+
+PLAN = ("cf0 cf1 nT cf2 cf3 nH cs2 cd0 cd1 cd2 nf1 nP ck0 cd3 nf2 ck1 cm0 nd0 cm2 cm1 nf0 cs3 ns2 cm3 nf3 cq nd1 ct nk0 nk1 nd2 ns3 nm0 nm1 nm2 nd3 nm3 "
+        "cu0 cu2 cu1 ca cn cx0 cg cu3 nq ce cx2 cx1 nt cx3 co cz cl nu0 cv na nu2 nn cr nu1 nx0 nu3 ng ne no ny2 nl nx1 ny3 nv nz nO cw nr nw")
+
+F8, U8, U16, BF, F32, I32 = "float8_e4m3fn_x4", "uint8", "uint16", "bfloat16", "float32", "int32"
+SCRATCH = {}
+for _n, _w in dict(xin=4 * OWN, grin=4 * OWN, rtin=512, win=2048, ubin=2048, prin=512, vin=512, zt=512, e4=2048, kt=544,
+                   cb=128 * NV, cn=128 * NV, rm=128 * NV, jk=2048, rsw=512, gg=256, gt=256, zz=512, bign=2912, bigc=2912).items():
+    SCRATCH[_n] = ("sbuf", [128, _w], BF)
+for _n, _w in dict(own=2 * OWN, rt=128, rp=128, ww=512, uu=512, pp=128, pq=128, vv=128, ee=512, kk=136, pk=768, hd=96, hr=16, cam=256,
+                   zp=256, zq=128, lxn=192, lgn=192, mmn=192, ddn=192, ohn=128, rrn=64, lxc=192, lgc=192, mmc=192, ddc=192, ohc=128, rrc=64).items():
+    SCRATCH[_n + "c"] = ("sbuf", [128, _w], F8)
+    SCRATCH[_n + "s"] = ("sbuf", [128, _w], U8)
+for _n, _w in dict(off=48, offg=16, fo=16, hrl=2, lland=8, pon=4, poc=4, lln=4, llc=4).items():
+    SCRATCH[_n] = ("sbuf", [128, _w], U16)
+for _n, _w in dict(st=160, fn=512, fc=512, yo=128).items():
+    SCRATCH[_n] = ("sbuf", [128, _w], F32)
+for _i in range(8):
+    SCRATCH["ps%d" % _i] = ("psum", [128, 512], F32)
+VIEW = {}
+for _b, _d, _l in (("ii", I32, "ip8 ic8 ra8 jj8 ta8 tb8 ua8 ub8 uc8 sc8 ka8 kb8 kq8 qi8 ci8 eb8 ec8 ed8 ef8"),
+                   ("lu", U16, "la8 lb8 lc8 ld8"),
+                   ("kf", F32, "klo8 kh8 khx8 kix8 mk8 kthr8 kr16 kk16 nk16 cse32 rs32"),
+                   ("kb", BF, "vals128 its128 idn128 ones128 wm96"),
+                   ("df", F32, "xd32 xo32 va32 vb32 iab64 vab64 vac32 vad16 vae8 xa16 pfa32 pra32 pfb32 prb32 vf40 vr40"),
+                   ("db", BF, "fb128 ft128 cum128 ctr128 nla32 nlb32 nra32 nrb32 nl32 nr32 np32"),
+                   ("hf", F32, "cf32 cft32 cfa8 cfb8")):
+    _o = 0
+    for _t in _l.split():
+        _n = _t.rstrip("0123456789")
+        VIEW[_n] = (_b, _o, int(_t[len(_n):]))
+        _o += int(_t[len(_n):])
+    SCRATCH[_b] = ("sbuf", [128, _o], _d)
+
+SEMAPHORES = ["vq", "sq", "tq", "gq", "ldx", "ldrt", "ldgr", "ldpr", "ldw", "ldu", "ldv", "selfcp", "outs", "outs2", "loc",
+              "hci", "hsi", "hli", "hri", "hrsi", "cxo", "cgo", "csc", "nxo", "ngo", "nsc", "rlc", "rcc", "rsc", "rln", "rcn", "rsn"]
+
+
+def roads(T, topo):
+    cores = [int(c) for c in T.cores]
+    cross = [[e for e in range(N) if e != q and not topo.may_write(cores[q], cores[e])] for q in range(N)]
+    road = {}
+    for q in range(N):
+        for e in cross[q]:
+            cq, ce = cores[q], cores[e]
+            if topo.die(cq) == topo.die(ce):
+                hs = [h for h in topo.cores_of(cq) if h != cq and topo.die(h) == topo.die(cq) and topo.may_write(h, ce)]
+                k = [f for f in cross[q] if topo.die(cores[f]) == topo.die(cq)].index(e)
+            else:
+                hs = [h for h in range(SIM) if topo.mates(h, ce) and topo.die(h) == topo.die(ce) and topo.may_write(cq, h) and topo.may_write(h, ce)]
+                k = [s for s in cross[e] if topo.die(cores[s]) != topo.die(ce)].index(q)
+            road[(q, e)] = hs[k % len(hs)]
+    return cores, cross, road
+
+
+def bits(es):
+    return sum(1 << e for e in es)
+
+
+def by(v):
+    return v.bitcast(dt.uint8)
+
+
+def w4(v):
+    return v.bitcast(dt.uint32)
+
+
+def hand_on(g, core, T, topo):
+    cores, cross, road = roads(T, topo)
+    mine = [k for k, h in road.items() if h == core]
+    if not mine:
+        return
+    q, e = mine[0]
+    ce = cores[e]
+    rid, pid = topo.addr(ce, core)
+    es = topo.engines(core, ce)
+    al, hs = bits(es), (bits(es[:len(es) // 2]), bits(es[len(es) // 2:]))
+    k = cross[e].index(q)
+    a = k * CAPP
+    g.wait_ge(T.sem.hsi, 4)
+    g.remote_dma_fused([RemoteDMATransfer(dst_ids=[DstId(rid=rid, pnc=pid)], dma_engine_mask=m, remote_sem=T.sem.csc, src=s, dst=d)
+                        for m, s, d in ((hs[0], T.hds[:, 0:48], T.lxcs[:, a:a + 48]), (hs[1], T.hds[:, 48:96], T.lgcs[:, a:a + 48]))], local_sem=T.sem.loc)
+    b = 16 * k
+    for sem, rsem, src, to in (("hci", "cxo", by(T.hdc[:, 0:48]), by(T.lxcc[:, a:a + 48])),
+                               ("hci", "cgo", by(T.hdc[:, 48:96]), by(T.lgcc[:, a:a + 48])),
+                               ("hli", "rlc", T.hrl[:, 0:1], T.lland[:, k:k + 1]),
+                               ("hri", "rcc", by(T.hrc[:]), by(T.camc[:, b:b + 16])),
+                               ("hrsi", "rsc", T.hrs[:], T.cams[:, b:b + 16])):
+        if rsem != "cgo":
+            g.wait_ge(T.sem[sem], 4)
+        g.remote_dma(to, src, T.sem[rsem], T.sem.loc, pid, rid, al)
+    g.wait_ge(T.sem.loc, 6 * len(es))
+
+
+def rank_program(g, core, T, topo):
+    me = T.rank_of(core)
+    if me is None:
+        return hand_on(g, core, T, topo)
+    cores, cross_all, road = roads(T, topo)
+    cross = cross_all[me]
+    near_of = lambda r: [s for s in range(N) if s != r and s not in cross_all[r]]
+    near = near_of(me)
+    onchip = lambda a, b: cores[b] in topo.cores_of(cores[a])
+    seat = lambda r: near_of(r)[:2] + [r] + near_of(r)[2:]
+
+    eng = {"vq": g.vector, "sq": g.scalar, "tq": g.tensor, "gq": g, "sync": g.sync}
+    cnt = {"vq": 0, "sq": 0, "tq": 0, "gq": 0}
+    seen = {q: {} for q in eng}
+
+    def wait(q, deps):
+        best = {}
+        for s, n in deps:
+            best[s] = max(best.get(s, 0), n)
+        for s, n in best.items():
+            if seen[q].get(s, 0) < n:
+                eng[q].wait_ge(T.sem[s], n)
+                seen[q][s] = n
+
+    def run(q, deps, fn, *a, **k):
+        wait(q, deps)
+        fn(*a, **k).then_inc(T.sem[q], 1)
+        cnt[q] += 1
+        return (q, cnt[q])
+
+    calls = {"copy": g.vector.tensor_copy, "tt": g.vector.tensor_tensor, "ts": g.vector.tensor_scalar,
+             "scan": g.vector.tensor_tensor_scan, "tr": g.vector.transpose, "set": g.vector.memset, "q": g.vector.quantize_mx}
+    V = lambda deps, name, *a, **k: run("vq", deps, calls[name], *a, **k)
+    S = lambda deps, *a, **k: run("sq", deps, g.scalar.activation, *a, **k)
+    G = lambda deps, fn, *a, **k: run("gq", deps, fn, *a, **k)
+    MM = lambda deps, out, l, r, a, b: run("tq", deps, g.tensor.matmul_mx, out, l[0], l[1], r[0], r[1], a, b)
+    used = [[] for _ in range(8)]
+    PS = [T["ps%d" % i] for i in range(8)]
+
+    def C(n, a=0, b=None, st=1):
+        buf, s, w = VIEW[n]
+        b = w if b is None else b
+        return T[buf][:, s + a:s + b] if st == 1 else T[buf][:, s + a:s + b:st]
+
+    def qp(n, a=0, b=None):
+        c, s = T[n + "c"], T[n + "s"]
+        b = c.shape[1] if b is None else b
+        return c[:, a:b], s[:, a:b]
+
+    def quant(deps, n, a, b, tile):
+        c, s = qp(n, a, b)
+        return V(deps, "q", c, s, tile)
+
+    def pickq(deps, to, frm, o):
+        return V(deps, "copy", w4(to[0]), w4(frm[0]).indirect(o)), S(deps, to[1], frm[1].indirect(o), AF.Copy)
+
+    def load(q, sem, out, in_):
+        q.dma_start(out, in_).then_inc(T.sem[sem], 16)
+        return (sem, 16)
+    lx = load(g.sync, "ldx", T.xin[:, 0:512], T.x[:])
+    lrt = load(g.scalar, "ldrt", T.rtin[:, 0:32], T.rt[:, 0:32])
+    lgr = load(g.sync, "ldgr", T.grin[:, 0:512], T.gr[:])
+    lpr = load(g.scalar, "ldpr", T.prin[:, 0:32], T.pr[:, 0:32])
+    lw = load(g.sync, "ldw", T.win[:], T.w[:])
+    lu = load(g.sync, "ldu", T.ubin[:], T.ub[:])
+    lv = load(g.scalar, "ldv", T.vin[:], T.v[:])
+
+    flags = dict(allow_small_or_imprecise_dtypes=True)
+    iota = lambda n, pat, base, cm: G([], g.iota, C(n), pat, base, cm, **flags)
+    gip = G([], g.iota, C("ip"), [[0, 8]], 0, 1)
+    gic = G([], g.iota, C("ic"), [[16, 8]], 0, 0)
+    gkr = iota("kr", [[1, 16]], 0, 0)
+    grm = G([], g.iota, T.rm[:], [[0, 128 * NV]], 1, 0, **flags)
+    grm = G([grm], g.iota, T.rm[:, 0:128 * NV:128], [[0, NV]], 0, 0, **flags)
+    gon = iota("ones", [[0, 128]], 1, 0)
+    gid = G([gon], g.affine_select, C("idn"), C("ones"), [[-1, 128]], OP.is_equal, 0.0, 0, 1)
+    gva = iota("vals", [[1, 128]], 0, 0)
+    gcs = iota("cse", [[0, 4], [64, 8]], -1, 0)
+    gi2 = iota("its", [[0, 8], [-2, 16]], 46, 0)
+    gci = G([], g.iota, C("ci"), [[0, 2], [1, 4]], 0, 0)
+    vz = V([], "set", T.zt[:], 0.0)
+    fill = lambda out: S([vz], out, T.zt[:, 0:out.shape[1]], AF.Copy)
+    frt = fill(T.rtin[:, 32:512])
+    fe = [fill(T.e4[:, 0:512])]
+    ra = V([gip], "ts", C("ra"), C("ip"), 15, None, OP.bitwise_and)
+    vr1 = V([], "set", C("rs"), BIG)
+    jj = V([ra, gic], "tt", C("jj"), C("ra"), C("ic"), OP.add)
+    vr2 = V([vr1], "set", C("rs", 0, 32, 8), -BIG)
+    eb = V([jj], "ts", C("eb"), C("jj"), 2, 7, OP.logical_shift_right, OP.bitwise_and)
+    ta = V([jj], "ts", C("ta"), C("jj"), 3, None, OP.bitwise_and)
+    ec = V([eb], "ts", C("ec"), C("eb"), -2, 7, OP.mult, OP.add)
+    tb = V([ta], "ts", C("tb"), C("ta"), 1, None, OP.is_equal)
+    kq = V([gip], "ts", C("kq"), C("ip"), 3, None, OP.bitwise_and)
+    ed = V([ec, tb], "tt", C("ed"), C("ec"), C("tb"), OP.mult)
+    sc = V([jj], "ts", C("sc"), C("jj"), 2, None, OP.logical_shift_right)
+    ef = V([ed], "tt", C("ef"), C("ed"), C("eb"), OP.add)
+    kt = V([kq], "ts", C("kthr"), C("kq"), 16, None, OP.mult)
+    l1 = V([ef], "copy", C("lb"), C("ef"))
+    l3 = V([sc], "copy", C("ld"), C("sc"))
+    vxt = V([], "set", T.xin[:, 512:4 * OWN], 0.0)
+    vs1 = V([], "set", T.st[:, 0:32], 0.0)
+    kk = S([kt, gkr], C("kk"), C("kr"), AF.Identity, bias=C("kthr", 0, 1))
+    nk = S([kk], C("nk"), C("kk"), AF.Copy, scale=-1.0, bias=-0.5)
+
+    qrt = quant([lrt, frt], "rt", 0, 128, T.rtin[:])
+    prt, prs = pickq([qrt, l1], qp("rp"), qp("rt"), C("lb"))
+    qx = quant([lx, vxt], "own", 0, OWN, T.xin[:])
+    ms = MM([prt, prs, qx], PS[0][:, 0:128], qp("rp"), qp("own", 0, 128), True, True)
+    ua = V([jj], "ts", C("ua"), C("jj"), 7, None, OP.bitwise_and)
+    vs2 = [V([], "set", C(n, 0, 8), 0.0) for n in ("vf", "vr")][1]
+    ub = V([ua], "ts", C("ub"), C("ua"), -2, 7, OP.mult, OP.add)
+    uc = V([ub], "tt", C("uc"), C("ub"), C("jj"), OP.add)
+    l2 = V([uc], "copy", C("lc"), C("uc"))
+    fe += [fill(T.e4[:, 512 * i:512 * i + 512]) for i in (1, 2, 3)]
+    fpr = fill(T.prin[:, 32:512])
+    tr = V([ms, vs1], "tr", T.st[:, 32:160], PS[0][:, 0:128])
+    used[0] = [tr]
+    X = [T.st[:, 32 + u:160:4] for u in range(2)]
+    p1 = [V([tr, vr2], "scan", C(("pfa", "pra")[u]), T.st[:, 28 + u:156:4], C("rs"), 0.0, OP.max, OP.min) for u in range(2)]
+    v3 = [V([p1[u], vs2], "tt", C(("vf", "vr")[u], 8, 40), X[u], C(("pfa", "pra")[u]), OP.min) for u in range(2)]
+    c1 = V([p1[0]], "tt", C("nla"), C("pfa"), X[0], OP.is_ge)
+    c2 = V([p1[1]], "tt", C("nra"), C("pra"), X[1], OP.is_gt)
+    p2 = [V([v3[u]], "scan", C(("pfb", "prb")[u]), C(("vf", "vr")[u], 7, 39), C("rs"), 0.0, OP.max, OP.min) for u in range(2)]
+    c4 = V([p2[0]], "tt", C("nlb"), C("pfb"), X[0], OP.is_ge)
+    c3 = V([p2[1]], "tt", C("nrb"), C("prb"), X[1], OP.is_gt)
+    a2 = V([c1, c4], "tt", C("nl"), C("nla"), C("nlb"), OP.add)
+    a1 = V([c2, c3], "tt", C("nr"), C("nra"), C("nrb"), OP.add)
+    npn = V([a1, a2, l2], "tt", C("np"), C("nr").indirect(C("lc", 0, 2)), C("nl"), OP.add)
+    fb = V([npn, l3], "ts", C("fb"), C("np").indirect(C("ld")), 1.5, None, OP.is_lt)
+    ft = V([fb], "tr", C("ft"), C("fb"))
+    cum = V([ft, vz], "scan", C("cum"), C("ft"), T.zt[:, 0:128], 0.0, OP.add, OP.add)
+    sa = None
+    for r in range(NS):
+        sa = S([cum, nk], T.jk[:, 128 * r:128 * r + 128], C("cum"), AF.Sign, bias=C("nk", r, r + 1), accum_out=C("xa", r, r + 1))
+    d2, d3 = [S([sa], C("xd", h, h + NS), C("xa", 0, NS), AF.Copy, scale=-0.5, bias=64.0) for h in (0, 16)]
+    cm = None
+    for r in range(NS, 16):
+        k = 128 * (r - NS)
+        cm = V([cum, kk], "ts", T.cb[:, k:k + 128], C("cum"), C("kk", r, r + 1), None, OP.is_le)
+    sn = V([cm, grm], "scan", T.cn[:], T.rm[:], T.cb[:], 0.0, OP.mult, OP.add)
+    vgt = V([], "set", T.grin[:, 512:4 * OWN], 0.0)
+    qg = quant([lgr, vgt], "own", OWN, 2 * OWN, T.grin[:])
+    d1 = [V([sn], "copy", C("xd", h + NS, h + 16), T.cn[:, 127:128 * NV:128]) for h in (0, 16)][1]
+    xo = V([d1, d2, d3], "tr", C("xo"), C("xd"))
+    of = None
+    for c in range(3):
+        V([xo], "copy", T.off[:, c:48:6], C("xo", c, 32, 4))
+        of = V([xo], "ts", T.off[:, 3 + c:48:6], C("xo", c, 32, 4), float(OWN), None, OP.add)
+
+    def runs(es):
+        l = []
+        for e in sorted(es):
+            if l and l[-1][1] == e:
+                l[-1][1] = e + 1
+            else:
+                l.append([e, e + 1])
+        return [(qp("pk", 96 * lo, 96 * hi), T.off[:, 6 * lo:6 * hi]) for lo, hi in l]
+    ready, (oc, osc) = [of, qx, qg], qp("own")
+    scales_s = lambda r: S(ready, r[0][1], osc.indirect(r[1]), AF.Copy)
+    scales_v = lambda r: V(ready, "copy", r[0][1], osc.indirect(r[1]))
+    codes = lambda r: V(ready, "copy", w4(r[0][0]), w4(oc).indirect(r[1]))
+    rc, rn = runs(cross), runs(near + [me])
+    psc = [scales_v(r) if i % 2 else scales_s(r) for i, r in enumerate(rc)]
+    pc = [codes(r) for r in rc][-1]
+    nsc = [scales_s(r) for r in rn][-1]
+    nc = [codes(r) for r in rn][-1]
+    wait("sync", [nc, nsc])
+    k, m = 48 * 2, 96 * me
+    for out, in_ in ((by(T.lxnc[:, k:k + 48]), by(T.pkc[:, m:m + 48])), (by(T.lgnc[:, k:k + 48]), by(T.pkc[:, m + 48:m + 96])),
+                     (T.lxns[:, k:k + 48], T.pks[:, m:m + 48]), (T.lgns[:, k:k + 48], T.pks[:, m + 48:m + 96])):
+        g.sync.dma_start(out, in_).then_inc(T.sem.selfcp, 16)
+
+    offe = topo.engines(core, [cores[e] for e in near if not onchip(me, e)][0])
+    one = [x for x in topo.engines(core, [cores[e] for e in near if onchip(me, e)][0]) if x not in offe]
+    loc = [0]
+
+    def fused(trs):
+        l = []
+        for d, es, s, a, b in trs:
+            rid, pid = topo.addr(d, core)
+            l.append(RemoteDMATransfer(dst_ids=[DstId(rid=rid, pnc=pid)], dma_engine_mask=bits(es), remote_sem=T.sem[s], src=a, dst=b))
+            loc[0] += len(es)
+        g.remote_dma_fused(l, local_sem=T.sem.loc)
+
+    hop, nhop, ka, kb = {}, {}, 0, 0
+    for e in cross:
+        h = road[(me, e)]
+        if h in topo.cores_of(core):
+            hop[e], ka = (h, one[ka:ka + 4]), ka + 4
+        else:
+            hop[e], kb = (h, offe[kb:kb + 4]), kb + 4
+    kb = 0
+    for e in near:
+        if onchip(me, e):
+            nhop[e] = one
+        else:
+            nhop[e], kb = offe[kb:kb + 4], kb + 4
+    half = lambda l, i: l[len(l) // 2 * i:len(l) // 2 * (i + 1)]
+
+    wait("gq", psc)
+    fused([(*hop[e], "hsi", T.pks[:, 96 * e:96 * e + 96], T.hds[:]) for e in cross])
+    wait("gq", [pc])
+    fused([(*hop[e], "hci", by(T.pkc[:, 96 * e:96 * e + 96]), by(T.hdc[:])) for e in cross])
+    at = lambda e: 48 * seat(e).index(me)
+    two = [(e, i, 96 * e + 48 * i, ("lxn", "lgn")[i]) for e in near for i in range(2)]
+    wait("gq", [nsc])
+    fused([(cores[e], half(nhop[e], i), "nsc", T.pks[:, p:p + 48], T[b + "s"][:, at(e):at(e) + 48]) for e, i, p, b in two])
+    wait("gq", [nc])
+    for k in range(2):
+        fused([(cores[e], nhop[e], ("nxo", "ngo")[k], by(T.pkc[:, p:p + 48]), by(T[b + "c"][:, at(e):at(e) + 48])) for e, i, p, b in two if i == k])
+
+    ie = [S([gid, fe[i]], T.e4[:, 512 * i + i:512 * i + 512:4], C("idn"), AF.Copy) for i in range(4)][-1]
+    o, p = VIEW["wm"][1], VIEW["ones"][1]
+    gwm = gci
+    for a in range(0, 128, 32):
+        gwm = G([gon, gwm], g.affine_select, T.kb[a:a + 32, o:o + 96], T.kb[a:a + 32, p:p + 96], [[32, 2], [-1, 48]], OP.not_equal, -1.0, 0, 1)
+    qw = quant([lw], "ww", 0, 512, T.win[:])
+    qe = quant([ie], "ee", 0, 512, T.e4[:])
+    vl0 = V([], "set", C("la"), 0)
+    vset = [V([], "set", T["f" + b][:, 48:64], -1.0) for b in "nc"][-1]
+    qpr = quant([lpr, fpr], "pp", 0, 128, T.prin[:])
+    pp, pps = pickq([qpr, vl0], qp("pq"), qp("pp"), C("la"))
+    fk = [fill(T.kt[:, 0:512]), fill(T.kt[:, 512:544])][-1]
+    foh = [fill(T["big" + b][:, 2304:2816]) for b in "nc"][-1]
+    vrs = S([vz], T.rsw[:], T.zt[:], AF.Identity, bias=128.0)
+    qu = quant([lu], "uu", 0, 512, T.ubin[:])
+    k1 = V([gip], "ts", C("ka"), C("ip"), 31, None, OP.bitwise_and)
+    k2 = V([gip], "ts", C("kb"), C("ip"), 15, None, OP.bitwise_and)
+    k3 = V([gip], "ts", C("qi"), C("ip"), 5, None, OP.logical_shift_right)
+    hi = V([k1, k2], "tt", C("kh"), C("ka"), C("kb"), OP.subtract)
+    lo = V([k2], "copy", C("klo"), C("kb"))
+    mk = V([k3, gci], "tt", C("mk"), C("qi"), C("ci"), OP.is_equal)
+    ix = V([k3], "ts", C("kix"), C("qi"), 48.0, 32.0, OP.mult, OP.add)
+    hx = V([hi, k3], "ts", C("khx"), C("qi"), 48.0, C("kh", 0, 1), OP.mult, OP.add)
+
+    R, QUARTERS, free = {}, range(4), list(range(1, 8)) + [0]
+
+    def tables(b):
+        for c, w, d, s in ((0, 8, lo, C("klo", 0, 1)), (1, 8, lo, C("klo", 0, 1)), (32, 4, hx, C("khx", 0, 1)), (33, 4, ix, C("kix", 0, 1)),
+                           (48, 4, hi, C("kh", 0, 1)), (49, 4, mk, 32.0)):
+            kl = V([mk, d, fk], "ts", T.kt[:, c:c + 4 * w - c % 2:4], C("mk", 0, w), s, None, OP.mult)
+        R["kk"] = quant([kl], "kk", 0, 136, T.kt[:])
+        R["ct"] = V([cum], "tr", C("ctr"), C("cum"))
+
+    def token_places(b):
+        va = V([R["ct"]], "ts", C("va"), C("ctr", 0, 128, 4), 49.0, None, OP.min)
+        ia = V([npn], "ts", C("iab", 0, 32), C("np"), 0.0, None, OP.is_equal)
+        vb = V([va, gcs], "tt", C("vb"), C("va"), C("cse"), OP.add)
+        ib = V([npn], "ts", C("iab", 32, 64), C("np"), 1.0, None, OP.is_equal)
+        ma = V([vb, ia], "tt", C("vab", 0, 32), C("vb"), C("iab", 0, 32), OP.mult)
+        mb = V([vb, ib], "tt", C("vab", 32, 64), C("vb"), C("iab", 32, 64), OP.mult)
+        h1 = V([ma, mb], "tt", C("vac"), C("vab", 0, 64, 2), C("vab", 1, 64, 2), OP.add)
+        h2 = V([h1], "tt", C("vad"), C("vac", 0, 32, 2), C("vac", 1, 32, 2), OP.add)
+        h3 = V([h2], "tt", C("vae"), C("vad", 0, 16, 2), C("vad", 1, 16, 2), OP.add)
+        R["og"] = [V([h3], "copy", T.offg[:, u:16:2], C("vae")) for u in range(2)]
+
+    def home_tiles(b):
+        R["qv"] = quant([lv], "vv", 0, 128, T.vin[:])
+        R["qz"] = quant([vz], "cam", 128, 256, T.zt[:])
+        R["cf"] = V([], "set", C("cf"), 0.0)
+
+    near_in = [("nsc", 16), ("selfcp", 64)]
+    come = {"nf": near_in + [("nxo", 16)], "nd": near_in + [("ngo", 16)], "cf": [("cxo", 32), ("csc", 32)], "cd": [("cgo", 32), ("csc", 32)]}
+
+    def product(key, deps, l, r, n):
+        o = free.pop(0)
+        R[key] = MM(deps + used[o], PS[o][:, 0:n], l, r, True, True), o
+
+    def give(key, deps):
+        o = R[key][1]
+        used[o] = deps
+        free.append(o)
+
+    def forward(b, i):
+        product((b, "f", i), come[b + "f"] + [qw, qe], qp("ww", 128 * i, 128 * i + 128), qp("lx" + b), 192)
+
+    def unpack(b, i):
+        product((b, "d", i), come[b + "d"] + [qw, qe], qp("ee", 128 * i, 128 * i + 128), qp("lg" + b), 192)
+
+    def mask_s(b, i):
+        B, (f, o) = T["big" + b], R[b, "f", i]
+        m = B[:, 1536 + 192 * i:1728 + 192 * i]
+        s = S([f], m, PS[o][:, 0:192], AF.Sign)
+        give((b, "f", i), [s])
+        R[b, "k", i] = S([s], B[:, 192 * i:192 * i + 192], m, AF.Relu)
+
+    def mask_v(b, i):
+        f, o = R[b, "f", i]
+        R[b, "k", i] = V([f], "ts", T["big" + b][:, 192 * i:192 * i + 192], PS[o][:, 0:192], 0.0, None, OP.is_gt)
+        give((b, "f", i), [R[b, "k", i]])
+
+    def masked(b, i):
+        B, (d, o) = T["big" + b], R[b, "d", i]
+        R[b, "m", i] = V([R[b, "k", i], d], "tt", B[:, 768 + i:1536:4], PS[o][:, 0:192], B[:, 192 * i:192 * i + 192], OP.mult)
+        give((b, "d", i), [R[b, "m", i]])
+
+    def quant_m(b):
+        R[b, "qm"] = quant([R[b, "m", i] for i in QUARTERS], "mm" + b, 0, 192, T["big" + b][:, 768:1536])
+
+    def strengths(b):
+        product((b, "st"), [R[b, "qm"], pp, pps], qp("pq"), qp("mm" + b), 192)
+
+    def before_dx(b, i):
+        product((b, "u", i), [R[b, "qm"], qu], qp("uu", 128 * i, 128 * i + 128), qp("mm" + b), 192)
+
+    def sizes(b):
+        F, (st, o) = T["f" + b], R[b, "st"]
+        R[b, "ab"] = [S([st, vset], F[32 * a:32 * a + 32, 0:48], PS[o][32 * a:32 * a + 32, 48 * a:48 * a + 48], AF.Abs) for a in range(4)]
+        give((b, "st"), R[b, "ab"][-1:])
+
+    def turn(b):
+        F = T["f" + b]
+        R[b, "tn"] = V(R[b, "ab"], "tr", F[:, 64:128], F[:, 0:64])
+
+    def scaled(b, i, on_scalar):
+        B, (u, o) = T["big" + b], R[b, "u", i]
+        deps = [u] + [R[b, "k", j] for j in QUARTERS]
+        out, in_ = B[:, 1536 + i:2304:4], PS[o][:, 0:192]
+        R[b, "x", i] = S(deps, out, in_, AF.Copy, scale=0.0625) if on_scalar else V(deps, "ts", out, in_, 0.0625, None, OP.mult)
+        give((b, "u", i), [R[b, "x", i]])
+
+    def signs(b):
+        F = T["f" + b]
+        R[b, "sg"] = [S([R[b, "tn"]], F[:, 256 + 48 * t:304 + 48 * t], F[:, 0:48], AF.Sign, bias=F[:, 64 + 32 * t:65 + 32 * t], scale=-1.0,
+                        accum_out=F[:, 160 + t:161 + t]) for t in range(2)]
+
+    def equals(b):
+        B, F = T["big" + b], T["f" + b]
+        eq = [V([R[b, "tn"]], "ts", B[:, 2816 + 48 * t:2864 + 48 * t], F[:, 0:48], F[:, 64 + 32 * t:65 + 32 * t], None, OP.is_equal) for t in range(2)]
+        R[b, "er"] = [V([eq[t], gwm], "scan", F[:, 352 + 48 * t:400 + 48 * t], B[:, 2816 + 48 * t:2864 + 48 * t], C("wm", 48 * t, 48 * t + 48), 0.0, OP.add, OP.mult)
+                      for t in range(2)]
+
+    def one_hot(b):
+        B, F = T["big" + b], T["f" + b]
+        oh = [V([R[b, "er"][t], R[b, "sg"][t], gi2, foh], "ts", B[:, 2304 + t:2816:4], C("its"), F[:, 160 + t:161 + t], F[:, 399 + 48 * t:400 + 48 * t],
+                OP.subtract, OP.is_equal) for t in range(2)]
+        R[b, "oh"] = quant(oh, "oh" + b, 0, 128, B[:, 2304:2816])
+
+    def lists(b):
+        o = free.pop(0)
+        MM([R[b, "oh"], R["kk"]] + used[o], PS[o][:, 0:128], qp("oh" + b), qp("kk", 0, 128), True, False)
+        R[b, "l"] = MM([], PS[o][:, 0:128], qp("oh" + b), qp("kk", 8, 136), False, True), o
+
+    def quant_dx(b):
+        R[b, "qd"] = quant([R[b, "x", i] for i in QUARTERS], "dd" + b, 0, 192, T["big" + b][:, 1536:2304])
+
+    def entries(b):
+        l, o = R[b, "l"]
+        R[b, "ll"] = V([l], "ts", T["ll" + b][:], PS[o][:, 4:8], 64.0 * me, None, OP.add)
+        R[b, "po"] = V([l], "copy", T["po" + b][:], PS[o][:, 0:4])
+        give((b, "l"), [R[b, "ll"], R[b, "po"]])
+
+    def answers(b):
+        R[b, "rc"], R[b, "rs"] = pickq([R[b, "qd"], R[b, "po"]], qp("rr" + b), qp("dd" + b), T["po" + b][:])
+
+    def own_answers(b):
+        R["own"] = pickq([R[b, "qd"], R[b, "po"]], qp("cam", 112, 128), qp("dd" + b), T["po" + b][:, 2:3])
+
+    def send(b):
+        to, rr, rs, ll = (cross, T.rrcc, T.rrcs, T.llc) if b == "c" else (near, T.rrnc, T.rrns, T.lln)
+        seats = [(e, i) if b == "c" else (e, seat(me).index(e)) for i, e in enumerate(to)]
+        k = lambda e: near_of(e).index(me)
+        for name, hsem, nsem, src, hland, land in (
+                ("ll", "hli", "rln", lambda i: ll[:, i:i + 1], T.hrl[:, 0:1], lambda e: T.lland[:, 4 + k(e):5 + k(e)]),
+                ("rc", "hri", "rcn", lambda i: by(rr[:, 16 * i:16 * i + 16]), by(T.hrc[:]), lambda e: by(T.camc[:, 64 + 16 * k(e):80 + 16 * k(e)])),
+                ("rs", "hrsi", "rsn", lambda i: rs[:, 16 * i:16 * i + 16], T.hrs[:], lambda e: T.cams[:, 64 + 16 * k(e):80 + 16 * k(e)])):
+            wait("gq", [R[b, name]])
+            fused([(*hop[e], hsem, src(i), hland) if b == "c" else (cores[e], nhop[e], nsem, src(i), land(e)) for e, i in seats])
+
+    stage = {"f": forward, "d": unpack, "s": mask_s, "k": mask_v, "m": masked, "q": quant_m, "t": strengths, "u": before_dx, "a": sizes, "n": turn,
+             "x": lambda b, i: scaled(b, i, True), "y": lambda b, i: scaled(b, i, False), "g": signs, "e": equals, "o": one_hot, "l": lists,
+             "z": quant_dx, "v": entries, "r": answers, "w": send, "O": own_answers, "T": tables, "P": token_places, "H": home_tiles}
+    for s in PLAN.split():
+        stage[s[1]](s[0], *[int(i) for i in s[2:]])
+    og1, og2 = R["og"]
+    qv, qzc, vcf, (own, owns), lln = R["qv"], R["qz"], R["cf"], R["own"], R["n", "ll"]
+
+    sc1 = V([vrs, lln, gva], "copy", T.rsw[:].indirect(T.lln[:, 2:3]), C("vals", 112, 128))
+    sc2 = V([sc1, ("rln", 16)], "copy", T.rsw[:].indirect(T.lland[:, 4:7]), C("vals", 64, 112))
+    sc3 = V([sc2, ("rlc", 32)], "copy", T.rsw[:].indirect(T.lland[:, 0:4]), C("vals", 0, 64))
+    arr = [("rcn", 16), ("rsn", 16), ("rcc", 32), ("rsc", 32), qzc, own, owns]
+    part = lambda h, w: slice(w * h, w * h + w)
+    gather = lambda h: V([sc3, og1, og2], "copy", T.gg[:, part(h, 128)], T.rsw[:].indirect(T.offg[:, part(h, 8)]))
+    turned = lambda h, d: V([d], "tr", T.gt[:, part(h, 128)], T.gg[:, part(h, 128)])
+    offsets = lambda h, d: V([d], "copy", T.fo[:, part(h, 8)], T.gt[:, 128 * h:128 * h + 128:16])
+    picked = lambda h, d: pickq(arr + [d], qp("zp", 128 * h, 128 * h + 128), qp("cam"), T.fo[:, part(h, 8)])
+    foa = offsets(0, turned(0, gather(0)))
+    gb = gather(1)
+    za = picked(0, foa)
+    gt = turned(1, gb)
+    zb = picked(1, offsets(1, gt))
+    f1 = V([gt], "ts", C("cfa"), T.gt[:, 0:128:16], 127.5, None, OP.is_lt)
+    f2 = V([gt], "ts", C("cfb"), T.gt[:, 128:256:16], 127.5, 2.0, OP.is_lt, OP.mult)
+    f3 = V([f1, f2, vcf], "tt", C("cf", 0, 8), C("cfa"), C("cfb"), OP.add)
+    f4 = V([f3], "tr", C("cft"), C("cf"))
+    wait("sync", [f4])
+    hf, o = VIEW["cft"][:2]
+    g.sync.dma_start(T.ct[:], T[hf][0:8, o:o + 16]).then_inc(T.sem.outs, 16)
+    zt, home = [], free[:5]
+    for h, zh in enumerate((za, zb)):
+        for i in QUARTERS:
+            b = home[i]
+            o = PS[b][:, 0:128]
+            t = MM([*zh] + used[b], o, qp("ee", 128 * i, 128 * i + 128), qp("zp", 128 * h, 128 * h + 128), h == 0, h == 1)
+            if h:
+                zt.append(V([t], "copy", T.zz[:, i:512:4], o) if i % 2 else S([t], T.zz[:, i:512:4], o, AF.Copy))
+    zq = quant(zt, "zq", 0, 128, T.zz[:])
+    wait("sync", [zq])
+    wait("sq", [zq])
+    g.sync.dma_start(T.oc[:], by(T.zqc[:])).then_inc(T.sem.outs, 16)
+    for k in range(4):
+        (g.sync if k < 2 else g.scalar).dma_start(T.osc[4 * k:4 * k + 4, :], T.zqs[32 * k:32 * k + 4, :]).then_inc(T.sem["outs" if k < 2 else "outs2"], 16)
+    ym = MM([zq, qv] + used[home[4]], PS[home[4]][:, 0:128], qp("vv"), qp("zq"), True, True)
+    yc = V([ym], "copy", T.yo[:], PS[home[4]][:, 0:128])
+    wait("sync", [yc])
+    g.sync.dma_start(T.y[:], T.yo[:]).then_inc(T.sem.outs, 16)
+
+    for s in ("vq", "sq", "tq", "gq"):
+        wait("gq", [(s, cnt[s])])
+    wait("gq", [lx, lrt, lgr, lw, lpr, lu, lv, ("outs", 80), ("outs2", 32), ("loc", loc[0])])

@@ -5,35 +5,44 @@ OP, AF = AluOpType, ActivationFunctionType
 N, CAPP, CAPR = 8, 48, 16
 SIM = 256
 BIG = 9.0e29
-NS = 7
+NS = 8
 NV = 16 - NS
 OWN = 130
+FW, HOP, PAIRS = "a", 3, False
 
-PLAN = ("cf0 cf1 nT cf2 cf3 nH cs2 cd0 cd1 cd2 nf1 nP ck0 cd3 nf2 ck1 cm0 nd0 cm2 cm1 nf0 cs3 ns2 cm3 nf3 cq nd1 ct nk0 nk1 nd2 ns3 nm0 nm1 nm2 nd3 nm3 "
+PLAN = ("cf0 cf1 cf2 cf3 cs2 cd0 cd1 cd2 nf1 ck0 cd3 nf2 ck1 cm0 nd0 cm2 cm1 nf0 cs3 ns2 cm3 nf3 cq nd1 ct nk0 nk1 nd2 ns3 nm0 nm1 nm2 nd3 nm3 "
         "cu0 cu2 cu1 ca cn cx0 cg cu3 nq ce cx2 cx1 nt cx3 co cz cl nu0 cv na nu2 nn cr nu1 nx0 nu3 ng ne no ny2 nl nx1 ny3 nv nz nO cw nr nw")
+ORDER = ("1 0 7 16 8 18 23 2 9 30 19 26 28 20 29 25 21 32 22 24 31 33 34 3 17 50 52 10 4 11 5 51 12 13 53 14 6 15 35 37 36 54 55 38 57 56 60 58 61 59 62 27 63 64 65 66 "
+         "67 69 68 39 70 71 40 45 41 44 43 42 72 91 88 85 87 82 89 83 84 86 79 74 78 75 77 73 76 80 90 92 93 81 94 95 96 97 98 99 106 123 105 104 107 145 103 124 102 116 "
+         "122 111 100 101 142 112 113 114 135 138 49 48 141 110 137 47 46 108 136 140 115 125 121 150 144 148 127 187 117 129 126 146 133 118 139 134 128 119 131 152 151 "
+         "159 147 157 163 149 154 130 109 153 165 156 164 177 166 132 120 155 162 161 168 158 207 167 180 178 169 160 170 181 179 186 182 197 183 188 191 171 194 198 189 "
+         "184 185 190 192 195 202 196 204 193 143 199 209 210 200 172 201 206 203 214 208 205 212 211 215 213 216 217 218 219 220 222 221 228 224 223 229 230 231 234 227 "
+         "225 226 245 247 244 246 235 232 233 236 237 238 240 241 252 248 254 242 249 257 258 243 173 259 239 256 255 272 261 251 253 266 250 260 262 264 265 273 274 263 "
+         "267 268 269 275 174 280 281 277 278 271 276 279 282 175 283 176 285 284 286 270 287 292 288 291 293 289 294 295 296 290 303 297 300 306 298 301 304 307 302 299 "
+         "305 308 309 315 313 310 311 312 316 314 317")
 
 F8, U8, U16, BF, F32, I32 = "float8_e4m3fn_x4", "uint8", "uint16", "bfloat16", "float32", "int32"
 SCRATCH = {}
-for _n, _w in dict(xin=4 * OWN, grin=4 * OWN, rtin=512, win=2048, ubin=2048, prin=512, vin=512, zt=512, e4=2048, kt=544,
-                   cb=128 * NV, cn=128 * NV, rm=128 * NV, jk=2048, rsw=512, gg=256, gt=256, zz=512, bign=2912, bigc=2912).items():
+for _n, _w in dict(xin=4 * OWN, grin=4 * OWN, rtin=512, win=2048, ubin=2048, prin=32, prt=512, vin=512, zt=544, e4=2048, kt=544,
+                   cb=65 * NV + 1, cn=65 * NV + 1, jk=64 * NS, rsw=512, gg=256, gt=256, zz=512, bign=3712, bigc=3712).items():
     SCRATCH[_n] = ("sbuf", [128, _w], BF)
-for _n, _w in dict(own=2 * OWN, rt=128, rp=128, ww=512, uu=512, pp=128, pq=128, vv=128, ee=512, kk=136, pk=768, hd=96, hr=16, cam=256,
-                   zp=256, zq=128, lxn=192, lgn=192, mmn=192, ddn=192, ohn=128, rrn=64, lxc=192, lgc=192, mmc=192, ddc=192, ohc=128, rrc=64).items():
+for _n, _w in dict(own=2 * OWN, rt=128, rp=128, ww=512, uu=512, pq=128, vv=128, ee=512, kk=136, pk=768, hd=96, hr=32, cam=256, zp=256, zq=128,
+                   lxn=192, lgn=192, mmn=192, ddn=192, ohn=128, rrn=64, lxc=192, lgc=192, mmc=192, ddc=192, ohc=128, rrc=64).items():
     SCRATCH[_n + "c"] = ("sbuf", [128, _w], F8)
     SCRATCH[_n + "s"] = ("sbuf", [128, _w], U8)
-for _n, _w in dict(off=48, offg=16, fo=16, hrl=2, lland=8, pon=4, poc=4, lln=4, llc=4).items():
+for _n, _w in dict(off=48, ofs=4, offg=16, fo=16, hrl=2, lland=8, lln=8, llc=8).items():
     SCRATCH[_n] = ("sbuf", [128, _w], U16)
-for _n, _w in dict(st=160, fn=512, fc=512, yo=128).items():
+for _n, _w in dict(st=168, fn=512, fc=512, yo=128).items():
     SCRATCH[_n] = ("sbuf", [128, _w], F32)
 for _i in range(8):
     SCRATCH["ps%d" % _i] = ("psum", [128, 512], F32)
 VIEW = {}
-for _b, _d, _l in (("ii", I32, "ip8 ic8 ra8 jj8 ta8 tb8 ua8 ub8 uc8 sc8 ka8 kb8 kq8 qi8 ci8 eb8 ec8 ed8 ef8"),
-                   ("lu", U16, "la8 lb8 lc8 ld8"),
-                   ("kf", F32, "klo8 kh8 khx8 kix8 mk8 kthr8 kr16 kk16 nk16 cse32 rs32"),
-                   ("kb", BF, "vals128 its128 idn128 ones128 wm96"),
-                   ("df", F32, "xd32 xo32 va32 vb32 iab64 vab64 vac32 vad16 vae8 xa16 pfa32 pra32 pfb32 prb32 vf40 vr40"),
-                   ("db", BF, "fb128 ft128 cum128 ctr128 nla32 nlb32 nra32 nrb32 nl32 nr32 np32"),
+for _b, _d, _l in (("ii", I32, "ip8 ic8 ra8 jj8 ta8 tb8 tc8 td8 ua8 ub8 uc8 ud8 ka8 kb8 kq8 qi8 ci8 eb8"),
+                   ("lu", U16, "lb8 lc8"),
+                   ("kf", F32, "klo8 kh8 khx8 kix8 mk8 kthr8 kr40 kk40 cse32 rs32"),
+                   ("kb", BF, "vals128 its128 idn128 ones128 wm98"),
+                   ("df", F32, "xd32 xo32 xp64 va32 vb32 iab64 vab64 vac32 vad16 vae8 pfa40 pra40 pfb32 prb32"),
+                   ("db", BF, "fb128 ft128 cum128 ctr128 up64 nla32 nlb32 nra32 nrb32 nm32 nl32 nr32"),
                    ("hf", F32, "cf32 cft32 cfa8 cfb8")):
     _o = 0
     for _t in _l.split():
@@ -42,7 +51,7 @@ for _b, _d, _l in (("ii", I32, "ip8 ic8 ra8 jj8 ta8 tb8 ua8 ub8 uc8 sc8 ka8 kb8 
         _o += int(_t[len(_n):])
     SCRATCH[_b] = ("sbuf", [128, _o], _d)
 
-SEMAPHORES = ["vq", "sq", "tq", "gq", "ldx", "ldrt", "ldgr", "ldpr", "ldw", "ldu", "ldv", "selfcp", "outs", "outs2", "loc",
+SEMAPHORES = ["vq", "sq", "tq", "gq", "ldx", "ldrt", "ldgr", "ldpr", "ldw", "ldu", "ldv", "outs", "outs2", "loc",
               "hci", "hsi", "hli", "hri", "hrsi", "cxo", "cgo", "csc", "nxo", "ngo", "nsc", "rlc", "rcc", "rsc", "rln", "rcn", "rsn"]
 
 
@@ -81,25 +90,35 @@ def hand_on(g, core, T, topo):
     if not mine:
         return
     q, e = mine[0]
-    ce = cores[e]
-    rid, pid = topo.addr(ce, core)
-    es = topo.engines(core, ce)
-    al, hs = bits(es), (bits(es[:len(es) // 2]), bits(es[len(es) // 2:]))
-    k = cross[e].index(q)
-    a = k * CAPP
-    g.wait_ge(T.sem.hsi, 4)
-    g.remote_dma_fused([RemoteDMATransfer(dst_ids=[DstId(rid=rid, pnc=pid)], dma_engine_mask=m, remote_sem=T.sem.csc, src=s, dst=d)
-                        for m, s, d in ((hs[0], T.hds[:, 0:48], T.lxcs[:, a:a + 48]), (hs[1], T.hds[:, 48:96], T.lgcs[:, a:a + 48]))], local_sem=T.sem.loc)
-    b = 16 * k
-    for sem, rsem, src, to in (("hci", "cxo", by(T.hdc[:, 0:48]), by(T.lxcc[:, a:a + 48])),
-                               ("hci", "cgo", by(T.hdc[:, 48:96]), by(T.lgcc[:, a:a + 48])),
-                               ("hli", "rlc", T.hrl[:, 0:1], T.lland[:, k:k + 1]),
-                               ("hri", "rcc", by(T.hrc[:]), by(T.camc[:, b:b + 16])),
-                               ("hrsi", "rsc", T.hrs[:], T.cams[:, b:b + 16])):
-        if rsem != "cgo":
-            g.wait_ge(T.sem[sem], 4)
-        g.remote_dma(to, src, T.sem[rsem], T.sem.loc, pid, rid, al)
-    g.wait_ge(T.sem.loc, 6 * len(es))
+    es = topo.engines(core, cores[e])
+    lo, hi = es[:len(es) // 2], es[len(es) // 2:]
+    sent = [0]
+
+    def on(sem, n, trs):
+        if sem:
+            g.wait_ge(T.sem[sem], n)
+        l = []
+        for f, m, s, a, b in trs:
+            rid, pid = topo.addr(cores[f], core)
+            l.append(RemoteDMATransfer(dst_ids=[DstId(rid=rid, pnc=pid)], dma_engine_mask=bits(m), remote_sem=T.sem[s], src=a, dst=b))
+            sent[0] += len(m)
+        g.remote_dma_fused(l, local_sem=T.sem.loc)
+    a = cross[e].index(q) * CAPP
+    n = 2 if FW == "c" else 4
+    on("hsi", n, [(e, lo, "csc", T.hds[:, 0:48], T.lxcs[:, a:a + 48]), (e, hi, "csc", T.hds[:, 48:96], T.lgcs[:, a:a + 48])])
+    x, gr = ("cxo", by(T.hdc[:, 0:48]), by(T.lxcc[:, a:a + 48])), ("cgo", by(T.hdc[:, 48:96]), by(T.lgcc[:, a:a + 48]))
+    if HOP == 2:
+        on("hci", n, [(e, lo, *x), (e, hi, *gr)])
+    else:
+        on("hci", n, [(e, es, *x)])
+        on(None, 0, [(e, es, *gr)])
+    if not PAIRS or core in topo.cores_of(cores[q]):
+        to = [f for f in cross[q] if cores[f] in topo.cores_of(cores[e])] if PAIRS else [e]
+        for sem, rsem, src, dst in (("hli", "rlc", lambda i: T.hrl[:, i:i + 1], lambda k: T.lland[:, k:k + 1]),
+                                    ("hri", "rcc", lambda i: by(T.hrc[:, 16 * i:16 * i + 16]), lambda k: by(T.camc[:, 16 * k:16 * k + 16])),
+                                    ("hrsi", "rsc", lambda i: T.hrs[:, 16 * i:16 * i + 16], lambda k: T.cams[:, 16 * k:16 * k + 16])):
+            on(sem, 8 if PAIRS else 4, [(f, (lo, hi)[i] if PAIRS else es, rsem, src(i), dst(cross[f].index(q))) for i, f in enumerate(to)])
+    g.wait_ge(T.sem.loc, sent[0])
 
 
 def rank_program(g, core, T, topo):
@@ -111,26 +130,21 @@ def rank_program(g, core, T, topo):
     near_of = lambda r: [s for s in range(N) if s != r and s not in cross_all[r]]
     near = near_of(me)
     onchip = lambda a, b: cores[b] in topo.cores_of(cores[a])
-    seat = lambda r: near_of(r)[:2] + [r] + near_of(r)[2:]
+    seat = lambda r: [r] + near_of(r)
 
     eng = {"vq": g.vector, "sq": g.scalar, "tq": g.tensor, "gq": g, "sync": g.sync}
-    cnt = {"vq": 0, "sq": 0, "tq": 0, "gq": 0}
-    seen = {q: {} for q in eng}
+    noted = []
 
-    def wait(q, deps):
-        best = {}
-        for s, n in deps:
-            best[s] = max(best.get(s, 0), n)
-        for s, n in best.items():
-            if seen[q].get(s, 0) < n:
-                eng[q].wait_ge(T.sem[s], n)
-                seen[q][s] = n
+    def flat(l):
+        return [x for d in l for x in (flat(d) if isinstance(d, list) else [d])]
 
     def run(q, deps, fn, *a, **k):
-        wait(q, deps)
-        fn(*a, **k).then_inc(T.sem[q], 1)
-        cnt[q] += 1
-        return (q, cnt[q])
+        noted.append((q, flat(deps), fn, a, k, q))
+        return len(noted) - 1
+
+    def dma(q, deps, sem, out, in_):
+        noted.append((q, flat(deps), eng[q].dma_start, (out, in_), {}, sem))
+        return (sem, 16)
 
     calls = {"copy": g.vector.tensor_copy, "tt": g.vector.tensor_tensor, "ts": g.vector.tensor_scalar,
              "scan": g.vector.tensor_tensor_scan, "tr": g.vector.transpose, "set": g.vector.memset, "q": g.vector.quantize_mx}
@@ -146,6 +160,10 @@ def rank_program(g, core, T, topo):
         b = w if b is None else b
         return T[buf][:, s + a:s + b] if st == 1 else T[buf][:, s + a:s + b:st]
 
+    def back(n, a, b):
+        buf, s, w = VIEW[n]
+        return T[buf][:, s + b - 1:s + a - 1:-1]
+
     def qp(n, a=0, b=None):
         c, s = T[n + "c"], T[n + "s"]
         b = c.shape[1] if b is None else b
@@ -156,100 +174,86 @@ def rank_program(g, core, T, topo):
         return V(deps, "q", c, s, tile)
 
     def pickq(deps, to, frm, o):
-        return V(deps, "copy", w4(to[0]), w4(frm[0]).indirect(o)), S(deps, to[1], frm[1].indirect(o), AF.Copy)
+        return [V(deps, "copy", w4(to[0]), w4(frm[0]).indirect(o)), S(deps, to[1], frm[1].indirect(o), AF.Copy)]
 
-    def load(q, sem, out, in_):
-        q.dma_start(out, in_).then_inc(T.sem[sem], 16)
-        return (sem, 16)
-    lx = load(g.sync, "ldx", T.xin[:, 0:512], T.x[:])
-    lrt = load(g.scalar, "ldrt", T.rtin[:, 0:32], T.rt[:, 0:32])
-    lgr = load(g.sync, "ldgr", T.grin[:, 0:512], T.gr[:])
-    lpr = load(g.scalar, "ldpr", T.prin[:, 0:32], T.pr[:, 0:32])
-    lw = load(g.sync, "ldw", T.win[:], T.w[:])
-    lu = load(g.sync, "ldu", T.ubin[:], T.ub[:])
-    lv = load(g.scalar, "ldv", T.vin[:], T.v[:])
+    lx = dma("sync", [], "ldx", T.xin[:, 0:512], T.x[:])
+    lrt = dma("sq", [], "ldrt", T.rtin[:, 0:32], T.rt[:, 0:32])
+    lgr = dma("sync", [], "ldgr", T.grin[:, 0:512], T.gr[:])
+    lpr = dma("sq", [], "ldpr", T.prin[:], T.pr[:, 0:32])
+    lw = dma("sync", [], "ldw", T.win[:], T.w[:])
+    lu = dma("sync", [], "ldu", T.ubin[:], T.ub[:])
+    lv = dma("sync", [], "ldv", T.vin[:], T.v[:])
 
     flags = dict(allow_small_or_imprecise_dtypes=True)
     iota = lambda n, pat, base, cm: G([], g.iota, C(n), pat, base, cm, **flags)
     gip = G([], g.iota, C("ip"), [[0, 8]], 0, 1)
     gic = G([], g.iota, C("ic"), [[16, 8]], 0, 0)
-    gkr = iota("kr", [[1, 16]], 0, 0)
-    grm = G([], g.iota, T.rm[:], [[0, 128 * NV]], 1, 0, **flags)
-    grm = G([grm], g.iota, T.rm[:, 0:128 * NV:128], [[0, NV]], 0, 0, **flags)
+    gkr = iota("kr", [[1, 40]], 0, 0)
     gon = iota("ones", [[0, 128]], 1, 0)
     gid = G([gon], g.affine_select, C("idn"), C("ones"), [[-1, 128]], OP.is_equal, 0.0, 0, 1)
-    gva = iota("vals", [[1, 128]], 0, 0)
-    gcs = iota("cse", [[0, 4], [64, 8]], -1, 0)
-    gi2 = iota("its", [[0, 8], [-2, 16]], 46, 0)
     gci = G([], g.iota, C("ci"), [[0, 2], [1, 4]], 0, 0)
+    gcs = iota("cse", [[0, 4], [64, 8]], -1, 0)
+    gva = iota("vals", [[1, 128]], 0, 0)
+    gi2 = iota("its", [[0, 8], [-2, 16]], 46, 0)
     vz = V([], "set", T.zt[:], 0.0)
     fill = lambda out: S([vz], out, T.zt[:, 0:out.shape[1]], AF.Copy)
     frt = fill(T.rtin[:, 32:512])
-    fe = [fill(T.e4[:, 0:512])]
     ra = V([gip], "ts", C("ra"), C("ip"), 15, None, OP.bitwise_and)
     vr1 = V([], "set", C("rs"), BIG)
     jj = V([ra, gic], "tt", C("jj"), C("ra"), C("ic"), OP.add)
     vr2 = V([vr1], "set", C("rs", 0, 32, 8), -BIG)
     eb = V([jj], "ts", C("eb"), C("jj"), 2, 7, OP.logical_shift_right, OP.bitwise_and)
-    ta = V([jj], "ts", C("ta"), C("jj"), 3, None, OP.bitwise_and)
-    ec = V([eb], "ts", C("ec"), C("eb"), -2, 7, OP.mult, OP.add)
-    tb = V([ta], "ts", C("tb"), C("ta"), 1, None, OP.is_equal)
     kq = V([gip], "ts", C("kq"), C("ip"), 3, None, OP.bitwise_and)
-    ed = V([ec, tb], "tt", C("ed"), C("ec"), C("tb"), OP.mult)
-    sc = V([jj], "ts", C("sc"), C("jj"), 2, None, OP.logical_shift_right)
-    ef = V([ed], "tt", C("ef"), C("ed"), C("eb"), OP.add)
-    kt = V([kq], "ts", C("kthr"), C("kq"), 16, None, OP.mult)
-    l1 = V([ef], "copy", C("lb"), C("ef"))
-    l3 = V([sc], "copy", C("ld"), C("sc"))
+    l1 = V([eb], "copy", C("lb"), C("eb"))
+    kt = V([kq], "ts", C("kthr"), C("kq"), 32, None, OP.mult)
     vxt = V([], "set", T.xin[:, 512:4 * OWN], 0.0)
-    vs1 = V([], "set", T.st[:, 0:32], 0.0)
+    vgt = V([], "set", T.grin[:, 512:4 * OWN], 0.0)
+    vs1, vs2, vs3 = [V([], "set", v, 0.0) for v in (T.st[:, 28:168:132], C("pfa", 0, 80, 72), C("fb", 3, 128, 4))]
+    vcb = V([], "set", T.cb[:, 0:65 * NV:65], 512.0)
+    ta = V([jj], "ts", C("ta"), C("jj"), 43, None, OP.mult)
+    ua = V([jj], "ts", C("ua"), C("jj"), 86, None, OP.mult)
+    tb = V([ta], "ts", C("tb"), C("ta"), 8, None, OP.logical_shift_right)
+    ub = V([ua], "ts", C("ub"), C("ua"), 8, None, OP.logical_shift_right)
+    tc = V([tb], "ts", C("tc"), C("tb"), -60, None, OP.mult)
+    uc = V([ub], "ts", C("uc"), C("ub"), 29, None, OP.mult)
+    td = V([tc, jj], "tt", C("td"), C("tc"), C("jj"), OP.add)
+    ud = V([td, uc], "tt", C("ud"), C("td"), C("uc"), OP.add)
+    l2 = V([ud], "copy", C("lc"), C("ud"))
     kk = S([kt, gkr], C("kk"), C("kr"), AF.Identity, bias=C("kthr", 0, 1))
-    nk = S([kk], C("nk"), C("kk"), AF.Copy, scale=-1.0, bias=-0.5)
+    fe = [fill(T.e4[:, 512 * i:512 * i + 512]) for i in range(4)]
+    ie = [S([gid, fe[i]], T.e4[:, 512 * i + i:512 * i + 512:4], C("idn"), AF.Copy) for i in range(4)]
 
     qrt = quant([lrt, frt], "rt", 0, 128, T.rtin[:])
-    prt, prs = pickq([qrt, l1], qp("rp"), qp("rt"), C("lb"))
+    prt = pickq([qrt, l1], qp("rp"), qp("rt"), C("lb"))
     qx = quant([lx, vxt], "own", 0, OWN, T.xin[:])
-    ms = MM([prt, prs, qx], PS[0][:, 0:128], qp("rp"), qp("own", 0, 128), True, True)
-    ua = V([jj], "ts", C("ua"), C("jj"), 7, None, OP.bitwise_and)
-    vs2 = [V([], "set", C(n, 0, 8), 0.0) for n in ("vf", "vr")][1]
-    ub = V([ua], "ts", C("ub"), C("ua"), -2, 7, OP.mult, OP.add)
-    uc = V([ub], "tt", C("uc"), C("ub"), C("jj"), OP.add)
-    l2 = V([uc], "copy", C("lc"), C("uc"))
-    fe += [fill(T.e4[:, 512 * i:512 * i + 512]) for i in (1, 2, 3)]
-    fpr = fill(T.prin[:, 32:512])
-    tr = V([ms, vs1], "tr", T.st[:, 32:160], PS[0][:, 0:128])
+    ms = MM([prt, qx], PS[0][:, 0:128], qp("rp"), qp("own", 0, 128), True, True)
+    tr = V([ms], "tr", T.st[:, 32:160], PS[0][:, 0:128])
     used[0] = [tr]
-    X = [T.st[:, 32 + u:160:4] for u in range(2)]
-    p1 = [V([tr, vr2], "scan", C(("pfa", "pra")[u]), T.st[:, 28 + u:156:4], C("rs"), 0.0, OP.max, OP.min) for u in range(2)]
-    v3 = [V([p1[u], vs2], "tt", C(("vf", "vr")[u], 8, 40), X[u], C(("pfa", "pra")[u]), OP.min) for u in range(2)]
-    c1 = V([p1[0]], "tt", C("nla"), C("pfa"), X[0], OP.is_ge)
-    c2 = V([p1[1]], "tt", C("nra"), C("pra"), X[1], OP.is_gt)
-    p2 = [V([v3[u]], "scan", C(("pfb", "prb")[u]), C(("vf", "vr")[u], 7, 39), C("rs"), 0.0, OP.max, OP.min) for u in range(2)]
-    c4 = V([p2[0]], "tt", C("nlb"), C("pfb"), X[0], OP.is_ge)
-    c3 = V([p2[1]], "tt", C("nrb"), C("prb"), X[1], OP.is_gt)
-    a2 = V([c1, c4], "tt", C("nl"), C("nla"), C("nlb"), OP.add)
-    a1 = V([c2, c3], "tt", C("nr"), C("nra"), C("nrb"), OP.add)
-    npn = V([a1, a2, l2], "tt", C("np"), C("nr").indirect(C("lc", 0, 2)), C("nl"), OP.add)
-    fb = V([npn, l3], "ts", C("fb"), C("np").indirect(C("ld")), 1.5, None, OP.is_lt)
-    ft = V([fb], "tr", C("ft"), C("fb"))
+    X, before, behind = T.st[:, 32:160:4], T.st[:, 28:156:4], T.st[:, 160:32:-4]
+    pf = V([tr, vr2, vs1], "scan", C("pfa", 1, 33), before, C("rs"), 0.0, OP.max, OP.min)
+    pr = V([tr, vr2, vs1], "scan", back("pra", 0, 32), behind, C("rs"), 0.0, OP.max, OP.min)
+    qf = V([pf, vs2], "scan", C("pfb"), before, C("pfa", 0, 32), 0.0, OP.max, OP.min)
+    qr = V([pr, vs2], "scan", back("prb", 0, 32), behind, back("pra", 1, 33), 0.0, OP.max, OP.min)
+    c2 = V([pr], "tt", C("nra"), C("pra", 0, 32), X, OP.is_le)
+    c1 = V([pf], "tt", C("nla"), C("pfa", 1, 33), X, OP.is_ge)
+    c4 = V([qf], "tt", C("nlb"), C("pfb"), X, OP.is_ge)
+    c3 = V([qr], "tt", C("nrb"), C("prb"), X, OP.is_le)
+    m1 = V([c4, c2], "tt", C("nm"), C("nlb"), C("nra"), OP.is_ge)
+    n2 = V([c3, c2], "tt", C("nr"), C("nra"), C("nrb"), OP.max)
+    n1 = V([m1, c1], "tt", C("nl"), C("nla"), C("nm"), OP.min)
+    fb = [V([n1, n2], "tt", C("fb", c, 128, 4), C("nr"), C("nl"), OP.is_gt) for c in range(3)]
+    ft = V([fb, vs3], "tr", C("ft"), C("fb"))
     cum = V([ft, vz], "scan", C("cum"), C("ft"), T.zt[:, 0:128], 0.0, OP.add, OP.add)
-    sa = None
-    for r in range(NS):
-        sa = S([cum, nk], T.jk[:, 128 * r:128 * r + 128], C("cum"), AF.Sign, bias=C("nk", r, r + 1), accum_out=C("xa", r, r + 1))
-    d2, d3 = [S([sa], C("xd", h, h + NS), C("xa", 0, NS), AF.Copy, scale=-0.5, bias=64.0) for h in (0, 16)]
-    cm = None
-    for r in range(NS, 16):
-        k = 128 * (r - NS)
-        cm = V([cum, kk], "ts", T.cb[:, k:k + 128], C("cum"), C("kk", r, r + 1), None, OP.is_le)
-    sn = V([cm, grm], "scan", T.cn[:], T.rm[:], T.cb[:], 0.0, OP.mult, OP.add)
-    vgt = V([], "set", T.grin[:, 512:4 * OWN], 0.0)
+    up = V([cum], "tt", back("up", 0, 64), C("cum", 0, 128, 2), C("cum", 1, 128, 2), OP.add)
+    sa = [S([up, kk], T.jk[:, 64 * r:64 * r + 64], C("up"), AF.Sign, bias=C("kk", 2 * r + 1, 2 * r + 2), scale=-1.0, accum_out=C("xd", r, r + 1)) for r in range(NS)]
+    d2 = S([sa], C("xd", 16, 16 + NS), C("xd", 0, NS), AF.Copy)
+    cm = [V([up, kk], "ts", T.cb[:, 65 * r + 1:65 * r + 65], C("up"), C("kk", 2 * (NS + r) + 2, 2 * (NS + r) + 3), -2.0, OP.subtract, OP.max) for r in range(NV)]
+    sn = V([cm, vcb, vz], "scan", T.cn[:, 0:65 * NV], T.cb[:, 0:65 * NV], T.zt[:, 0:65 * NV], 0.0, OP.add, OP.min)
     qg = quant([lgr, vgt], "own", OWN, 2 * OWN, T.grin[:])
-    d1 = [V([sn], "copy", C("xd", h + NS, h + 16), T.cn[:, 127:128 * NV:128]) for h in (0, 16)][1]
-    xo = V([d1, d2, d3], "tr", C("xo"), C("xd"))
-    of = None
-    for c in range(3):
-        V([xo], "copy", T.off[:, c:48:6], C("xo", c, 32, 4))
-        of = V([xo], "ts", T.off[:, 3 + c:48:6], C("xo", c, 32, 4), float(OWN), None, OP.add)
+    d1 = [V([sn], "ts", C("xd", h + NS, h + 16), T.cn[:, 64:65 * NV:65], -1.0, -64.0, OP.mult, OP.add) for h in (0, 16)]
+    xo = V([d1, d2], "tr", C("xo"), C("xd"))
+    xp = [V([xo], "ts", C("xp", 32 * u, 32 * u + 32), C("xo"), 64.0 + OWN * u, None, OP.add) for u in range(2)]
+    of = V([xp, l2], "copy", T.off[:], C("xp").indirect(C("lc", 0, 3)))
 
     def runs(es):
         l = []
@@ -258,33 +262,30 @@ def rank_program(g, core, T, topo):
                 l[-1][1] = e + 1
             else:
                 l.append([e, e + 1])
-        return [(qp("pk", 96 * lo, 96 * hi), T.off[:, 6 * lo:6 * hi]) for lo, hi in l]
+        return [(qp("pk", 96 * lo, 96 * hi), T.off[:, 6 * lo:6 * hi]) for lo, hi in sorted(l, key=lambda r: r[0] - r[1])]
     ready, (oc, osc) = [of, qx, qg], qp("own")
     scales_s = lambda r: S(ready, r[0][1], osc.indirect(r[1]), AF.Copy)
     scales_v = lambda r: V(ready, "copy", r[0][1], osc.indirect(r[1]))
     codes = lambda r: V(ready, "copy", w4(r[0][0]), w4(oc).indirect(r[1]))
-    rc, rn = runs(cross), runs(near + [me])
-    psc = [scales_v(r) if i % 2 else scales_s(r) for i, r in enumerate(rc)]
-    pc = [codes(r) for r in rc][-1]
-    nsc = [scales_s(r) for r in rn][-1]
-    nc = [codes(r) for r in rn][-1]
-    wait("sync", [nc, nsc])
-    k, m = 48 * 2, 96 * me
-    for out, in_ in ((by(T.lxnc[:, k:k + 48]), by(T.pkc[:, m:m + 48])), (by(T.lgnc[:, k:k + 48]), by(T.pkc[:, m + 48:m + 96])),
-                     (T.lxns[:, k:k + 48], T.pks[:, m:m + 48]), (T.lgns[:, k:k + 48], T.pks[:, m + 48:m + 96])):
-        g.sync.dma_start(out, in_).then_inc(T.sem.selfcp, 16)
+    rc, rn = runs(cross), runs(near)
+    psc = [scales_s(rc[0]), scales_v(rc[1])]
+    nsc = [scales_s(rn[0]), (scales_v if FW == "c" else scales_s)(rn[1])]
+    pc = [codes(r) for r in rc]
+    nc = [codes(r) for r in rn]
+    o2 = V([xp], "copy", T.ofs[:, 0:3], C("xp", 32 + 4 * me, 35 + 4 * me))
+    mine = [pickq(ready, qp("lxn", 0, 48), qp("own"), T.off[:, 6 * me:6 * me + 3]), pickq(ready + [o2], qp("lgn", 0, 48), qp("own"), T.ofs[:, 0:3])]
 
     offe = topo.engines(core, [cores[e] for e in near if not onchip(me, e)][0])
     one = [x for x in topo.engines(core, [cores[e] for e in near if onchip(me, e)][0]) if x not in offe]
     loc = [0]
 
-    def fused(trs):
+    def fused(deps, trs):
         l = []
         for d, es, s, a, b in trs:
             rid, pid = topo.addr(d, core)
             l.append(RemoteDMATransfer(dst_ids=[DstId(rid=rid, pnc=pid)], dma_engine_mask=bits(es), remote_sem=T.sem[s], src=a, dst=b))
             loc[0] += len(es)
-        g.remote_dma_fused(l, local_sem=T.sem.loc)
+        noted.append(("gq", flat(deps), g.remote_dma_fused, (l,), dict(local_sem=T.sem.loc), None))
 
     hop, nhop, ka, kb = {}, {}, 0, 0
     for e in cross:
@@ -300,75 +301,77 @@ def rank_program(g, core, T, topo):
         else:
             nhop[e], kb = offe[kb:kb + 4], kb + 4
     half = lambda l, i: l[len(l) // 2 * i:len(l) // 2 * (i + 1)]
-
-    wait("gq", psc)
-    fused([(*hop[e], "hsi", T.pks[:, 96 * e:96 * e + 96], T.hds[:]) for e in cross])
-    wait("gq", [pc])
-    fused([(*hop[e], "hci", by(T.pkc[:, 96 * e:96 * e + 96]), by(T.hdc[:])) for e in cross])
     at = lambda e: 48 * seat(e).index(me)
     two = [(e, i, 96 * e + 48 * i, ("lxn", "lgn")[i]) for e in near for i in range(2)]
-    wait("gq", [nsc])
-    fused([(cores[e], half(nhop[e], i), "nsc", T.pks[:, p:p + 48], T[b + "s"][:, at(e):at(e) + 48]) for e, i, p, b in two])
-    wait("gq", [nc])
-    for k in range(2):
-        fused([(cores[e], nhop[e], ("nxo", "ngo")[k], by(T.pkc[:, p:p + 48]), by(T[b + "c"][:, at(e):at(e) + 48])) for e, i, p, b in two if i == k])
+    ns_ = lambda es: [(cores[e], es(e, i), "nsc", T.pks[:, p:p + 48], T[b + "s"][:, at(e):at(e) + 48]) for e, i, p, b in two]
+    nc_ = lambda es, ks: [(cores[e], es(e, i), ("nxo", "ngo")[i], by(T.pkc[:, p:p + 48]), by(T[b + "c"][:, at(e):at(e) + 48])) for e, i, p, b in two if i in ks]
+    halves = lambda e, i: half(nhop[e], i)
+    if FW == "c":
+        ce = lambda e, i: hop[e][1][i:i + 1]
+        ne = lambda e, i: nhop[e][2 + 4 * i:4 + 4 * i] if onchip(me, e) else nhop[e][2 + i:3 + i]
+        fused([psc, nsc], [(hop[e][0], ce(e, i), "hsi", T.pks[:, 96 * e + 48 * i:96 * e + 48 * i + 48], T.hds[:, 48 * i:48 * i + 48]) for e in cross for i in range(2)] + ns_(ne))
+        fused([pc, nc], [(hop[e][0], ce(e, i), "hci", by(T.pkc[:, 96 * e + 48 * i:96 * e + 48 * i + 48]), by(T.hdc[:, 48 * i:48 * i + 48])) for e in cross for i in range(2)]
+              + nc_(ne, (0, 1)))
+    else:
+        fused(psc, [(*hop[e], "hsi", T.pks[:, 96 * e:96 * e + 96], T.hds[:]) for e in cross])
+        fused(pc, [(*hop[e], "hci", by(T.pkc[:, 96 * e:96 * e + 96]), by(T.hdc[:])) for e in cross])
+        fused(nsc, ns_(halves))
+        if FW == "b":
+            fused(nc, nc_(halves, (0, 1)))
+        else:
+            for k in range(2):
+                fused(nc, nc_(lambda e, i: nhop[e], (k,)))
+    n_s, n_c = {"a": (16, 16), "b": (16, 8), "c": (8, 4)}[FW]
 
-    ie = [S([gid, fe[i]], T.e4[:, 512 * i + i:512 * i + 512:4], C("idn"), AF.Copy) for i in range(4)][-1]
     o, p = VIEW["wm"][1], VIEW["ones"][1]
-    gwm = gci
+    gwm = V([gid], "set", C("ones", 48, 49), 0.0)
     for a in range(0, 128, 32):
-        gwm = G([gon, gwm], g.affine_select, T.kb[a:a + 32, o:o + 96], T.kb[a:a + 32, p:p + 96], [[32, 2], [-1, 48]], OP.not_equal, -1.0, 0, 1)
-    qw = quant([lw], "ww", 0, 512, T.win[:])
-    qe = quant([ie], "ee", 0, 512, T.e4[:])
-    vl0 = V([], "set", C("la"), 0)
-    vset = [V([], "set", T["f" + b][:, 48:64], -1.0) for b in "nc"][-1]
-    qpr = quant([lpr, fpr], "pp", 0, 128, T.prin[:])
-    pp, pps = pickq([qpr, vl0], qp("pq"), qp("pp"), C("la"))
-    fk = [fill(T.kt[:, 0:512]), fill(T.kt[:, 512:544])][-1]
-    foh = [fill(T["big" + b][:, 2304:2816]) for b in "nc"][-1]
-    vrs = S([vz], T.rsw[:], T.zt[:], AF.Identity, bias=128.0)
-    qu = quant([lu], "uu", 0, 512, T.ubin[:])
+        gwm = G([gwm], g.affine_select, T.kb[a:a + 32, o:o + 98], T.kb[a:a + 32, p:p + 98], [[32, 2], [-1, 49]], OP.not_equal, -1.0, 0, 1)
+    QUARTERS = range(4)
+    piece = lambda d, n, buf, i: quant(d, n, 128 * i, 128 * i + 128, buf[:, 512 * i:512 * i + 512])
+    qw = [piece([lw], "ww", T.win, i) for i in QUARTERS]
+    qe = [piece([ie[i]], "ee", T.e4, i) for i in QUARTERS]
+    qu = [piece([lu], "uu", T.ubin, i) for i in QUARTERS]
+    vset = {b: V([], "set", T["f" + b][:, 48:64], -1.0) for b in "nc"}
+    qpr = quant([S([lpr, vz], T.prt[:, t:512:4], T.zt[:, 0:128], AF.Identity, bias=T.prin[:, t:t + 1]) for t in QUARTERS], "pq", 0, 128, T.prt[:])
+    fk = fill(T.kt[:])
+    foh = {b: fill(T["big" + b][:, 2304:2816]) for b in "cn"}
+    vrs = S([vz], T.rsw[:], T.zt[:, 0:512], AF.Identity, bias=128.0)
     k1 = V([gip], "ts", C("ka"), C("ip"), 31, None, OP.bitwise_and)
-    k2 = V([gip], "ts", C("kb"), C("ip"), 15, None, OP.bitwise_and)
     k3 = V([gip], "ts", C("qi"), C("ip"), 5, None, OP.logical_shift_right)
-    hi = V([k1, k2], "tt", C("kh"), C("ka"), C("kb"), OP.subtract)
-    lo = V([k2], "copy", C("klo"), C("kb"))
+    hi = V([k1, ra], "tt", C("kh"), C("ka"), C("ra"), OP.subtract)
+    lo = V([ra], "copy", C("klo"), C("ra"))
     mk = V([k3, gci], "tt", C("mk"), C("qi"), C("ci"), OP.is_equal)
+    veq = {b: V([], "set", T["big" + b][:, 2864:2865], 0.0) for b in "nc"}
     ix = V([k3], "ts", C("kix"), C("qi"), 48.0, 32.0, OP.mult, OP.add)
     hx = V([hi, k3], "ts", C("khx"), C("qi"), 48.0, C("kh", 0, 1), OP.mult, OP.add)
+    kl = [V([mk, d, fk], "ts", T.kt[:, c:c + 4 * w - c % 2:4], C("mk", 0, w), s, None, OP.mult)
+          for c, w, d, s in ((0, 8, lo, C("klo", 0, 1)), (1, 8, lo, C("klo", 0, 1)), (32, 4, hx, C("khx", 0, 1)), (33, 4, ix, C("kix", 0, 1)),
+                             (48, 4, hi, C("kh", 0, 1)), (49, 4, mk, 32.0))]
+    qk = quant([kl, V([fk], "set", T.kt[0:1, 50:66:4], 64.0 * me)], "kk", 0, 136, T.kt[:])
+    ones = {b: V([foh[b]], "set", T["big" + b][0:1, 2306:2816:4], 1.0) for b in "cn"}
+    ct = V([cum], "tr", C("ctr"), C("cum"))
+    va = V([ct], "ts", C("va"), C("ctr", 0, 128, 4), 49.0, None, OP.min)
+    ia = V([c1, c2], "tt", C("iab", 0, 32), C("nra"), C("nla"), OP.is_gt)
+    vb = V([va, gcs], "tt", C("vb"), C("va"), C("cse"), OP.add)
+    ib = V([ia, fb], "tt", C("iab", 32, 64), C("fb", 0, 128, 4), C("iab", 0, 32), OP.subtract)
+    ma = V([vb, ia], "tt", C("vab", 0, 32), C("vb"), C("iab", 0, 32), OP.mult)
+    mb = V([vb, ib], "tt", C("vab", 32, 64), C("vb"), C("iab", 32, 64), OP.mult)
+    h1 = V([ma, mb], "tt", C("vac"), C("vab", 0, 64, 2), C("vab", 1, 64, 2), OP.add)
+    h2 = V([h1], "tt", C("vad"), C("vac", 0, 32, 2), C("vac", 1, 32, 2), OP.add)
+    h3 = V([h2], "tt", C("vae"), C("vad", 0, 16, 2), C("vad", 1, 16, 2), OP.add)
+    og = [V([h3], "copy", T.offg[:, u:16:2], C("vae")) for u in range(2)]
+    qv = quant([lv], "vv", 0, 128, T.vin[:])
+    qzc = quant([vz], "cam", 128, 256, T.zt[:, 0:512])
+    vcf = V([], "set", C("cf"), 0.0)
 
-    R, QUARTERS, free = {}, range(4), list(range(1, 8)) + [0]
+    R, free = {}, list(range(1, 8)) + [0]
+    n_h = 16 if HOP == 2 else 32
+    come = {"nf": [mine[0], ("nsc", n_s), ("nxo", n_c)], "nd": [mine[1], ("nsc", n_s), ("ngo", n_c)], "cf": [("csc", 32), ("cxo", n_h)], "cd": [("csc", 32), ("cgo", n_h)]}
 
-    def tables(b):
-        for c, w, d, s in ((0, 8, lo, C("klo", 0, 1)), (1, 8, lo, C("klo", 0, 1)), (32, 4, hx, C("khx", 0, 1)), (33, 4, ix, C("kix", 0, 1)),
-                           (48, 4, hi, C("kh", 0, 1)), (49, 4, mk, 32.0)):
-            kl = V([mk, d, fk], "ts", T.kt[:, c:c + 4 * w - c % 2:4], C("mk", 0, w), s, None, OP.mult)
-        R["kk"] = quant([kl], "kk", 0, 136, T.kt[:])
-        R["ct"] = V([cum], "tr", C("ctr"), C("cum"))
-
-    def token_places(b):
-        va = V([R["ct"]], "ts", C("va"), C("ctr", 0, 128, 4), 49.0, None, OP.min)
-        ia = V([npn], "ts", C("iab", 0, 32), C("np"), 0.0, None, OP.is_equal)
-        vb = V([va, gcs], "tt", C("vb"), C("va"), C("cse"), OP.add)
-        ib = V([npn], "ts", C("iab", 32, 64), C("np"), 1.0, None, OP.is_equal)
-        ma = V([vb, ia], "tt", C("vab", 0, 32), C("vb"), C("iab", 0, 32), OP.mult)
-        mb = V([vb, ib], "tt", C("vab", 32, 64), C("vb"), C("iab", 32, 64), OP.mult)
-        h1 = V([ma, mb], "tt", C("vac"), C("vab", 0, 64, 2), C("vab", 1, 64, 2), OP.add)
-        h2 = V([h1], "tt", C("vad"), C("vac", 0, 32, 2), C("vac", 1, 32, 2), OP.add)
-        h3 = V([h2], "tt", C("vae"), C("vad", 0, 16, 2), C("vad", 1, 16, 2), OP.add)
-        R["og"] = [V([h3], "copy", T.offg[:, u:16:2], C("vae")) for u in range(2)]
-
-    def home_tiles(b):
-        R["qv"] = quant([lv], "vv", 0, 128, T.vin[:])
-        R["qz"] = quant([vz], "cam", 128, 256, T.zt[:])
-        R["cf"] = V([], "set", C("cf"), 0.0)
-
-    near_in = [("nsc", 16), ("selfcp", 64)]
-    come = {"nf": near_in + [("nxo", 16)], "nd": near_in + [("ngo", 16)], "cf": [("cxo", 32), ("csc", 32)], "cd": [("cgo", 32), ("csc", 32)]}
-
-    def product(key, deps, l, r, n):
+    def product(key, deps, l, r):
         o = free.pop(0)
-        R[key] = MM(deps + used[o], PS[o][:, 0:n], l, r, True, True), o
+        R[key] = MM([deps, used[o]], PS[o][:, 0:192], l, r, True, True), o
 
     def give(key, deps):
         o = R[key][1]
@@ -376,14 +379,14 @@ def rank_program(g, core, T, topo):
         free.append(o)
 
     def forward(b, i):
-        product((b, "f", i), come[b + "f"] + [qw, qe], qp("ww", 128 * i, 128 * i + 128), qp("lx" + b), 192)
+        product((b, "f", i), [come[b + "f"], qw[i]], qp("ww", 128 * i, 128 * i + 128), qp("lx" + b))
 
     def unpack(b, i):
-        product((b, "d", i), come[b + "d"] + [qw, qe], qp("ee", 128 * i, 128 * i + 128), qp("lg" + b), 192)
+        product((b, "d", i), [come[b + "d"], qe[i]], qp("ee", 128 * i, 128 * i + 128), qp("lg" + b))
 
     def mask_s(b, i):
         B, (f, o) = T["big" + b], R[b, "f", i]
-        m = B[:, 1536 + 192 * i:1728 + 192 * i]
+        m = B[:, 2944 + 192 * i:3136 + 192 * i]
         s = S([f], m, PS[o][:, 0:192], AF.Sign)
         give((b, "f", i), [s])
         R[b, "k", i] = S([s], B[:, 192 * i:192 * i + 192], m, AF.Relu)
@@ -402,47 +405,45 @@ def rank_program(g, core, T, topo):
         R[b, "qm"] = quant([R[b, "m", i] for i in QUARTERS], "mm" + b, 0, 192, T["big" + b][:, 768:1536])
 
     def strengths(b):
-        product((b, "st"), [R[b, "qm"], pp, pps], qp("pq"), qp("mm" + b), 192)
+        product((b, "st"), [R[b, "qm"], qpr], qp("pq"), qp("mm" + b))
 
     def before_dx(b, i):
-        product((b, "u", i), [R[b, "qm"], qu], qp("uu", 128 * i, 128 * i + 128), qp("mm" + b), 192)
+        product((b, "u", i), [R[b, "qm"], qu[i]], qp("uu", 128 * i, 128 * i + 128), qp("mm" + b))
 
     def sizes(b):
         F, (st, o) = T["f" + b], R[b, "st"]
-        R[b, "ab"] = [S([st, vset], F[32 * a:32 * a + 32, 0:48], PS[o][32 * a:32 * a + 32, 48 * a:48 * a + 48], AF.Abs) for a in range(4)]
-        give((b, "st"), R[b, "ab"][-1:])
+        R[b, "ab"] = [S([st], F[32 * a:32 * a + 32, 0:48], PS[o][32 * a:32 * a + 32, 48 * a:48 * a + 48], AF.Abs) for a in range(4)]
+        give((b, "st"), R[b, "ab"])
 
     def turn(b):
         F = T["f" + b]
-        R[b, "tn"] = V(R[b, "ab"], "tr", F[:, 64:128], F[:, 0:64])
+        R[b, "tn"] = V([R[b, "ab"], vset[b]], "tr", F[:, 64:128], F[:, 0:64])
 
     def scaled(b, i, on_scalar):
         B, (u, o) = T["big" + b], R[b, "u", i]
-        deps = [u] + [R[b, "k", j] for j in QUARTERS]
         out, in_ = B[:, 1536 + i:2304:4], PS[o][:, 0:192]
-        R[b, "x", i] = S(deps, out, in_, AF.Copy, scale=0.0625) if on_scalar else V(deps, "ts", out, in_, 0.0625, None, OP.mult)
+        R[b, "x", i] = S([u], out, in_, AF.Copy, scale=0.0625) if on_scalar else V([u], "ts", out, in_, 0.0625, None, OP.mult)
         give((b, "u", i), [R[b, "x", i]])
 
     def signs(b):
         F = T["f" + b]
-        R[b, "sg"] = [S([R[b, "tn"]], F[:, 256 + 48 * t:304 + 48 * t], F[:, 0:48], AF.Sign, bias=F[:, 64 + 32 * t:65 + 32 * t], scale=-1.0,
+        R[b, "sg"] = [S([R[b, "tn"], R[b, "ab"]], F[:, 256 + 48 * t:304 + 48 * t], F[:, 0:48], AF.Sign, bias=F[:, 64 + 32 * t:65 + 32 * t], scale=-1.0,
                         accum_out=F[:, 160 + t:161 + t]) for t in range(2)]
 
     def equals(b):
         B, F = T["big" + b], T["f" + b]
-        eq = [V([R[b, "tn"]], "ts", B[:, 2816 + 48 * t:2864 + 48 * t], F[:, 0:48], F[:, 64 + 32 * t:65 + 32 * t], None, OP.is_equal) for t in range(2)]
-        R[b, "er"] = [V([eq[t], gwm], "scan", F[:, 352 + 48 * t:400 + 48 * t], B[:, 2816 + 48 * t:2864 + 48 * t], C("wm", 48 * t, 48 * t + 48), 0.0, OP.add, OP.mult)
-                      for t in range(2)]
+        eq = [V([R[b, "tn"]], "ts", B[:, 2816 + 49 * t:2864 + 49 * t], F[:, 0:48], F[:, 64 + 32 * t:65 + 32 * t], None, OP.is_equal) for t in range(2)]
+        R[b, "er"] = V([eq, gwm, veq[b]], "scan", F[:, 352:449], B[:, 2816:2913], C("wm", 0, 97), 0.0, OP.add, OP.mult)
 
     def one_hot(b):
         B, F = T["big" + b], T["f" + b]
-        oh = [V([R[b, "er"][t], R[b, "sg"][t], gi2, foh], "ts", B[:, 2304 + t:2816:4], C("its"), F[:, 160 + t:161 + t], F[:, 399 + 48 * t:400 + 48 * t],
+        oh = [V([R[b, "er"], R[b, "sg"][t], gi2, foh[b]], "ts", B[:, 2304 + t:2816:4], C("its"), F[:, 160 + t:161 + t], F[:, 399 + 49 * t:400 + 49 * t],
                 OP.subtract, OP.is_equal) for t in range(2)]
-        R[b, "oh"] = quant(oh, "oh" + b, 0, 128, B[:, 2304:2816])
+        R[b, "oh"] = quant([oh, ones[b]], "oh" + b, 0, 128, B[:, 2304:2816])
 
     def lists(b):
         o = free.pop(0)
-        MM([R[b, "oh"], R["kk"]] + used[o], PS[o][:, 0:128], qp("oh" + b), qp("kk", 0, 128), True, False)
+        MM([R[b, "oh"], qk, used[o]], PS[o][:, 0:128], qp("oh" + b), qp("kk", 0, 128), True, False)
         R[b, "l"] = MM([], PS[o][:, 0:128], qp("oh" + b), qp("kk", 8, 136), False, True), o
 
     def quant_dx(b):
@@ -450,75 +451,89 @@ def rank_program(g, core, T, topo):
 
     def entries(b):
         l, o = R[b, "l"]
-        R[b, "ll"] = V([l], "ts", T["ll" + b][:], PS[o][:, 4:8], 64.0 * me, None, OP.add)
-        R[b, "po"] = V([l], "copy", T["po" + b][:], PS[o][:, 0:4])
-        give((b, "l"), [R[b, "ll"], R[b, "po"]])
+        R[b, "ll"] = V([l], "copy", T["ll" + b][:], PS[o][:, 0:8])
+        give((b, "l"), [R[b, "ll"]])
 
     def answers(b):
-        R[b, "rc"], R[b, "rs"] = pickq([R[b, "qd"], R[b, "po"]], qp("rr" + b), qp("dd" + b), T["po" + b][:])
+        R[b, "rc"], R[b, "rs"] = pickq([R[b, "qd"], R[b, "ll"]], qp("rr" + b), qp("dd" + b), T["ll" + b][:, 0:4])
 
     def own_answers(b):
-        R["own"] = pickq([R[b, "qd"], R[b, "po"]], qp("cam", 112, 128), qp("dd" + b), T["po" + b][:, 2:3])
+        R["own"] = pickq([R[b, "qd"], R[b, "ll"]], qp("cam", 112, 128), qp("dd" + b), T["ll" + b][:, 0:1])
 
     def send(b):
-        to, rr, rs, ll = (cross, T.rrcc, T.rrcs, T.llc) if b == "c" else (near, T.rrnc, T.rrns, T.lln)
-        seats = [(e, i) if b == "c" else (e, seat(me).index(e)) for i, e in enumerate(to)]
+        rr, rs, ll = T["rr" + b + "c"], T["rr" + b + "s"], T["ll" + b]
         k = lambda e: near_of(e).index(me)
+        n = 2 if PAIRS else 1
         for name, hsem, nsem, src, hland, land in (
-                ("ll", "hli", "rln", lambda i: ll[:, i:i + 1], T.hrl[:, 0:1], lambda e: T.lland[:, 4 + k(e):5 + k(e)]),
-                ("rc", "hri", "rcn", lambda i: by(rr[:, 16 * i:16 * i + 16]), by(T.hrc[:]), lambda e: by(T.camc[:, 64 + 16 * k(e):80 + 16 * k(e)])),
-                ("rs", "hrsi", "rsn", lambda i: rs[:, 16 * i:16 * i + 16], T.hrs[:], lambda e: T.cams[:, 64 + 16 * k(e):80 + 16 * k(e)])):
-            wait("gq", [R[b, name]])
-            fused([(*hop[e], hsem, src(i), hland) if b == "c" else (cores[e], nhop[e], nsem, src(i), land(e)) for e, i in seats])
+                ("ll", "hli", "rln", lambda i, n: ll[:, 4 + i:4 + i + n], T.hrl[:, 0:n], lambda e: T.lland[:, 4 + k(e):5 + k(e)]),
+                ("rc", "hri", "rcn", lambda i, n: by(rr[:, 16 * i:16 * (i + n)]), by(T.hrc[:, 0:16 * n]), lambda e: by(T.camc[:, 64 + 16 * k(e):80 + 16 * k(e)])),
+                ("rs", "hrsi", "rsn", lambda i, n: rs[:, 16 * i:16 * (i + n)], T.hrs[:, 0:16 * n], lambda e: T.cams[:, 64 + 16 * k(e):80 + 16 * k(e)])):
+            if b == "n":
+                fused([R[b, name]], [(cores[e], nhop[e], nsem, src(seat(me).index(e), 1), land(e)) for e in near])
+            elif PAIRS:
+                here = [e for e in cross if hop[e][0] in topo.cores_of(core)]
+                fused([R[b, name]], [(hop[e][0], (offe, one)[i], hsem, src(cross.index(e) // 2 * 2, 2), hland) for i, e in enumerate(here)])
+            else:
+                fused([R[b, name]], [(*hop[e], hsem, src(i, 1), hland) for i, e in enumerate(cross)])
 
     stage = {"f": forward, "d": unpack, "s": mask_s, "k": mask_v, "m": masked, "q": quant_m, "t": strengths, "u": before_dx, "a": sizes, "n": turn,
              "x": lambda b, i: scaled(b, i, True), "y": lambda b, i: scaled(b, i, False), "g": signs, "e": equals, "o": one_hot, "l": lists,
-             "z": quant_dx, "v": entries, "r": answers, "w": send, "O": own_answers, "T": tables, "P": token_places, "H": home_tiles}
+             "z": quant_dx, "v": entries, "r": answers, "w": send, "O": own_answers}
     for s in PLAN.split():
         stage[s[1]](s[0], *[int(i) for i in s[2:]])
-    og1, og2 = R["og"]
-    qv, qzc, vcf, (own, owns), lln = R["qv"], R["qz"], R["cf"], R["own"], R["n", "ll"]
+    (own, owns), lln, n_r = R["own"], R["n", "ll"], 16 if PAIRS else 32
 
-    sc1 = V([vrs, lln, gva], "copy", T.rsw[:].indirect(T.lln[:, 2:3]), C("vals", 112, 128))
-    sc2 = V([sc1, ("rln", 16)], "copy", T.rsw[:].indirect(T.lland[:, 4:7]), C("vals", 64, 112))
-    sc3 = V([sc2, ("rlc", 32)], "copy", T.rsw[:].indirect(T.lland[:, 0:4]), C("vals", 0, 64))
-    arr = [("rcn", 16), ("rsn", 16), ("rcc", 32), ("rsc", 32), qzc, own, owns]
+    sc1 = V([vrs, lln, gva], "copy", T.rsw[:].indirect(T.lln[:, 4:5]), C("vals", 112, 128))
+    sc2 = V([sc1, ("rlc", n_r)], "copy", T.rsw[:].indirect(T.lland[:, 0:4]), C("vals", 0, 64))
+    sc3 = V([sc2, ("rln", 16)], "copy", T.rsw[:].indirect(T.lland[:, 4:7]), C("vals", 64, 112))
     part = lambda h, w: slice(w * h, w * h + w)
-    gather = lambda h: V([sc3, og1, og2], "copy", T.gg[:, part(h, 128)], T.rsw[:].indirect(T.offg[:, part(h, 8)]))
-    turned = lambda h, d: V([d], "tr", T.gt[:, part(h, 128)], T.gg[:, part(h, 128)])
-    offsets = lambda h, d: V([d], "copy", T.fo[:, part(h, 8)], T.gt[:, 128 * h:128 * h + 128:16])
-    picked = lambda h, d: pickq(arr + [d], qp("zp", 128 * h, 128 * h + 128), qp("cam"), T.fo[:, part(h, 8)])
-    foa = offsets(0, turned(0, gather(0)))
-    gb = gather(1)
-    za = picked(0, foa)
-    gt = turned(1, gb)
-    zb = picked(1, offsets(1, gt))
+    ga = V([sc3, og], "copy", T.gg[:, 0:128], T.rsw[:].indirect(T.offg[:, 0:8]))
+    gb = S([sc3, og], T.gg[:, 128:256], T.rsw[:].indirect(T.offg[:, 8:16]), AF.Copy)
+    gt = [V([d], "tr", T.gt[:, part(h, 128)], T.gg[:, part(h, 128)]) for h, d in enumerate((ga, gb))]
+    fo = V([gt], "copy", T.fo[:], T.gt[:, 0:256:16])
+    cc, cs = [("rcn", 16), ("rcc", n_r), qzc, own, fo], [("rsn", 16), ("rsc", n_r), qzc, owns, fo]
+    zc = [V(cc, "copy", w4(T.zpc[:, part(h, 128)]), w4(T.camc[:]).indirect(T.fo[:, part(h, 8)])) for h in range(2)]
+    zs = [S(cs, T.zps[:, 0:128], T.cams[:].indirect(T.fo[:, 0:8]), AF.Copy), V(cs, "copy", T.zps[:, 128:256], T.cams[:].indirect(T.fo[:, 8:16]))]
     f1 = V([gt], "ts", C("cfa"), T.gt[:, 0:128:16], 127.5, None, OP.is_lt)
     f2 = V([gt], "ts", C("cfb"), T.gt[:, 128:256:16], 127.5, 2.0, OP.is_lt, OP.mult)
     f3 = V([f1, f2, vcf], "tt", C("cf", 0, 8), C("cfa"), C("cfb"), OP.add)
     f4 = V([f3], "tr", C("cft"), C("cf"))
-    wait("sync", [f4])
     hf, o = VIEW["cft"][:2]
-    g.sync.dma_start(T.ct[:], T[hf][0:8, o:o + 16]).then_inc(T.sem.outs, 16)
+    dma("sync", [f4], "outs", T.ct[:], T[hf][0:8, o:o + 16])
     zt, home = [], free[:5]
-    for h, zh in enumerate((za, zb)):
-        for i in QUARTERS:
+    for i in QUARTERS:
+        for h in range(2):
             b = home[i]
             o = PS[b][:, 0:128]
-            t = MM([*zh] + used[b], o, qp("ee", 128 * i, 128 * i + 128), qp("zp", 128 * h, 128 * h + 128), h == 0, h == 1)
-            if h:
-                zt.append(V([t], "copy", T.zz[:, i:512:4], o) if i % 2 else S([t], T.zz[:, i:512:4], o, AF.Copy))
+            t = MM([zc[h], zs[h], qe[i], used[b]], o, qp("ee", 128 * i, 128 * i + 128), qp("zp", 128 * h, 128 * h + 128), h == 0, h == 1)
+        zt.append(V([t], "copy", T.zz[:, i:512:4], o) if i % 2 else S([t], T.zz[:, i:512:4], o, AF.Copy))
     zq = quant(zt, "zq", 0, 128, T.zz[:])
-    wait("sync", [zq])
-    wait("sq", [zq])
-    g.sync.dma_start(T.oc[:], by(T.zqc[:])).then_inc(T.sem.outs, 16)
+    dma("sync", [zq], "outs", T.oc[:], by(T.zqc[:]))
     for k in range(4):
-        (g.sync if k < 2 else g.scalar).dma_start(T.osc[4 * k:4 * k + 4, :], T.zqs[32 * k:32 * k + 4, :]).then_inc(T.sem["outs" if k < 2 else "outs2"], 16)
-    ym = MM([zq, qv] + used[home[4]], PS[home[4]][:, 0:128], qp("vv"), qp("zq"), True, True)
+        dma("sync" if k < 2 else "sq", [zq], "outs" if k < 2 else "outs2", T.osc[4 * k:4 * k + 4, :], T.zqs[32 * k:32 * k + 4, :])
+    ym = MM([zq, qv, used[home[4]]], PS[home[4]][:, 0:128], qp("vv"), qp("zq"), True, True)
     yc = V([ym], "copy", T.yo[:], PS[home[4]][:, 0:128])
-    wait("sync", [yc])
-    g.sync.dma_start(T.y[:], T.yo[:]).then_inc(T.sem.outs, 16)
+    dma("sq", [yc], "outs2", T.y[:], T.yo[:])
 
-    for s in ("vq", "sq", "tq", "gq"):
-        wait("gq", [(s, cnt[s])])
-    wait("gq", [lx, lrt, lgr, lw, lpr, lu, lv, ("outs", 80), ("outs2", 32), ("loc", loc[0])])
+    cnt, seen, done = {q: 0 for q in eng}, {q: {} for q in eng}, {}
+
+    def wait(q, deps):
+        best = {}
+        for s, n in deps:
+            best[s] = max(best.get(s, 0), n)
+        for s, n in best.items():
+            if seen[q].get(s, 0) < n:
+                eng[q].wait_ge(T.sem[s], n)
+                seen[q][s] = n
+
+    for i in [int(t) for t in ORDER.split()] or range(len(noted)):
+        q, deps, fn, a, k, sem = noted[i]
+        wait(q, [done[d] if isinstance(d, int) else d for d in deps])
+        call = fn(*a, **k)
+        if sem == q:
+            call.then_inc(T.sem[q], 1)
+            cnt[q] += 1
+            done[i] = (q, cnt[q])
+        elif sem:
+            call.then_inc(T.sem[sem], 16)
+    wait("gq", [(s, cnt[s]) for s in ("vq", "sq", "tq", "gq")] + [lx, lrt, lgr, lw, lpr, lu, lv, ("outs", 64), ("outs2", 48), ("loc", loc[0])])

from concourse.bass import DstId, RemoteDMATransfer
from concourse.mybir import dt, AluOpType, AxisListType, ActivationFunctionType

OP, AF = AluOpType, ActivationFunctionType
N, CAPP, CAPR = 8, 48, 16
SIM = 256
BIG = 9.0e29
NS = 8
NV = 16 - NS
OWN = 130
FW, HOP, PAIRS = "a", 3, False

PLAN = ("cf0 cf1 cf2 cf3 cs2 cd0 cd1 cd2 nf1 ck0 cd3 nf2 ck1 cm0 nd0 cm2 cm1 nf0 cs3 ns2 cm3 nf3 cq nd1 ct nk0 nk1 nd2 ns3 nm0 nm1 nm2 nd3 nm3 "
        "cu0 cu2 cu1 ca cn cx0 cg cu3 nq ce cx2 cx1 nt cx3 co cz cl nu0 cv na nu2 nn cr nu1 nx0 nu3 ng ne no ny2 nl nx1 ny3 nv nz nO cw nr nw")
ORDER = ("1 0 7 16 8 18 23 2 9 30 19 26 28 20 29 25 21 32 22 24 31 33 34 3 17 50 52 10 4 11 5 51 12 13 53 14 6 15 35 37 36 54 55 38 57 56 60 58 61 59 62 27 63 64 65 66 "
         "67 69 68 39 70 71 40 45 41 44 43 42 72 91 88 85 87 82 89 83 84 86 79 74 78 75 77 73 76 80 90 92 93 81 94 95 96 97 98 99 106 123 105 104 107 145 103 124 102 116 "
         "122 111 100 101 142 112 113 114 135 138 49 48 141 110 137 47 46 108 136 140 115 125 121 150 144 148 127 187 117 129 126 146 133 118 139 134 128 119 131 152 151 "
         "159 147 157 163 149 154 130 109 153 165 156 164 177 166 132 120 155 162 161 168 158 207 167 180 178 169 160 170 181 179 186 182 197 183 188 191 171 194 198 189 "
         "184 185 190 192 195 202 196 204 193 143 199 209 210 200 172 201 206 203 214 208 205 212 211 215 213 216 217 218 219 220 222 221 228 224 223 229 230 231 234 227 "
         "225 226 245 247 244 246 235 232 233 236 237 238 240 241 252 248 254 242 249 257 258 243 173 259 239 256 255 272 261 251 253 266 250 260 262 264 265 273 274 263 "
         "267 268 269 275 174 280 281 277 278 271 276 279 282 175 283 176 285 284 286 270 287 292 288 291 293 289 294 295 296 290 303 297 300 306 298 301 304 307 302 299 "
         "305 308 309 315 313 310 311 312 316 314 317")

F8, U8, U16, BF, F32, I32 = "float8_e4m3fn_x4", "uint8", "uint16", "bfloat16", "float32", "int32"
SCRATCH = {}
for _n, _w in dict(xin=4 * OWN, grin=4 * OWN, rtin=512, win=2048, ubin=2048, prin=32, prt=512, vin=512, zt=544, e4=2048, kt=544,
                   cb=65 * NV + 1, cn=65 * NV + 1, jk=64 * NS, rsw=512, gg=256, gt=256, zz=512, bign=3712, bigc=3712).items():
    SCRATCH[_n] = ("sbuf", [128, _w], BF)
for _n, _w in dict(own=2 * OWN, rt=128, rp=128, ww=512, uu=512, pq=128, vv=128, ee=512, kk=136, pk=768, hd=96, hr=32, cam=256, zp=256, zq=128,
                   lxn=192, lgn=192, mmn=192, ddn=192, ohn=128, rrn=64, lxc=192, lgc=192, mmc=192, ddc=192, ohc=128, rrc=64).items():
    SCRATCH[_n + "c"] = ("sbuf", [128, _w], F8)
    SCRATCH[_n + "s"] = ("sbuf", [128, _w], U8)
for _n, _w in dict(off=48, ofs=4, offg=16, fo=16, hrl=2, lland=8, lln=8, llc=8).items():
    SCRATCH[_n] = ("sbuf", [128, _w], U16)
for _n, _w in dict(st=168, fn=512, fc=512, yo=128).items():
    SCRATCH[_n] = ("sbuf", [128, _w], F32)
for _i in range(8):
    SCRATCH["ps%d" % _i] = ("psum", [128, 512], F32)
VIEW = {}
for _b, _d, _l in (("ii", I32, "ip8 ic8 ra8 jj8 ta8 tb8 tc8 td8 ua8 ub8 uc8 ud8 ka8 kb8 kq8 qi8 ci8 eb8"),
                   ("lu", U16, "lb8 lc8"),
                   ("kf", F32, "klo8 kh8 khx8 kix8 mk8 kthr8 kr40 kk40 cse32 rs32"),
                   ("kb", BF, "vals128 its128 idn128 ones128 wm98"),
                   ("df", F32, "xd32 xo32 xp64 va32 vb32 iab64 vab64 vac32 vad16 vae8 pfa40 pra40 pfb32 prb32"),
                   ("db", BF, "fb128 ft128 cum128 ctr128 up64 nla32 nlb32 nra32 nrb32 nm32 nl32 nr32"),
                   ("hf", F32, "cf32 cft32 cfa8 cfb8")):
    _o = 0
    for _t in _l.split():
        _n = _t.rstrip("0123456789")
        VIEW[_n] = (_b, _o, int(_t[len(_n):]))
        _o += int(_t[len(_n):])
    SCRATCH[_b] = ("sbuf", [128, _o], _d)

SEMAPHORES = ["vq", "sq", "tq", "gq", "ldx", "ldrt", "ldgr", "ldpr", "ldw", "ldu", "ldv", "outs", "outs2", "loc",
              "hci", "hsi", "hli", "hri", "hrsi", "cxo", "cgo", "csc", "nxo", "ngo", "nsc", "rlc", "rcc", "rsc", "rln", "rcn", "rsn"]


def roads(T, topo):
    cores = [int(c) for c in T.cores]
    cross = [[e for e in range(N) if e != q and not topo.may_write(cores[q], cores[e])] for q in range(N)]
    road = {}
    for q in range(N):
        for e in cross[q]:
            cq, ce = cores[q], cores[e]
            if topo.die(cq) == topo.die(ce):
                hs = [h for h in topo.cores_of(cq) if h != cq and topo.die(h) == topo.die(cq) and topo.may_write(h, ce)]
                k = [f for f in cross[q] if topo.die(cores[f]) == topo.die(cq)].index(e)
            else:
                hs = [h for h in range(SIM) if topo.mates(h, ce) and topo.die(h) == topo.die(ce) and topo.may_write(cq, h) and topo.may_write(h, ce)]
                k = [s for s in cross[e] if topo.die(cores[s]) != topo.die(ce)].index(q)
            road[(q, e)] = hs[k % len(hs)]
    return cores, cross, road


def bits(es):
    return sum(1 << e for e in es)


def by(v):
    return v.bitcast(dt.uint8)


def w4(v):
    return v.bitcast(dt.uint32)


def hand_on(g, core, T, topo):
    cores, cross, road = roads(T, topo)
    mine = [k for k, h in road.items() if h == core]
    if not mine:
        return
    q, e = mine[0]
    es = topo.engines(core, cores[e])
    lo, hi = es[:len(es) // 2], es[len(es) // 2:]
    sent = [0]

    def on(sem, n, trs):
        if sem:
            g.wait_ge(T.sem[sem], n)
        l = []
        for f, m, s, a, b in trs:
            rid, pid = topo.addr(cores[f], core)
            l.append(RemoteDMATransfer(dst_ids=[DstId(rid=rid, pnc=pid)], dma_engine_mask=bits(m), remote_sem=T.sem[s], src=a, dst=b))
            sent[0] += len(m)
        g.remote_dma_fused(l, local_sem=T.sem.loc)
    a = cross[e].index(q) * CAPP
    n = 2 if FW == "c" else 4
    on("hsi", n, [(e, lo, "csc", T.hds[:, 0:48], T.lxcs[:, a:a + 48]), (e, hi, "csc", T.hds[:, 48:96], T.lgcs[:, a:a + 48])])
    x, gr = ("cxo", by(T.hdc[:, 0:48]), by(T.lxcc[:, a:a + 48])), ("cgo", by(T.hdc[:, 48:96]), by(T.lgcc[:, a:a + 48]))
    if HOP == 2:
        on("hci", n, [(e, lo, *x), (e, hi, *gr)])
    else:
        on("hci", n, [(e, es, *x)])
        on(None, 0, [(e, es, *gr)])
    if not PAIRS or core in topo.cores_of(cores[q]):
        to = [f for f in cross[q] if cores[f] in topo.cores_of(cores[e])] if PAIRS else [e]
        for sem, rsem, src, dst in (("hli", "rlc", lambda i: T.hrl[:, i:i + 1], lambda k: T.lland[:, k:k + 1]),
                                    ("hri", "rcc", lambda i: by(T.hrc[:, 16 * i:16 * i + 16]), lambda k: by(T.camc[:, 16 * k:16 * k + 16])),
                                    ("hrsi", "rsc", lambda i: T.hrs[:, 16 * i:16 * i + 16], lambda k: T.cams[:, 16 * k:16 * k + 16])):
            on(sem, 8 if PAIRS else 4, [(f, (lo, hi)[i] if PAIRS else es, rsem, src(i), dst(cross[f].index(q))) for i, f in enumerate(to)])
    g.wait_ge(T.sem.loc, sent[0])


def rank_program(g, core, T, topo):
    me = T.rank_of(core)
    if me is None:
        return hand_on(g, core, T, topo)
    cores, cross_all, road = roads(T, topo)
    cross = cross_all[me]
    near_of = lambda r: [s for s in range(N) if s != r and s not in cross_all[r]]
    near = near_of(me)
    onchip = lambda a, b: cores[b] in topo.cores_of(cores[a])
    seat = lambda r: [r] + near_of(r)

    eng = {"vq": g.vector, "sq": g.scalar, "tq": g.tensor, "gq": g, "sync": g.sync}
    noted = []

    def flat(l):
        return [x for d in l for x in (flat(d) if isinstance(d, list) else [d])]

    def run(q, deps, fn, *a, **k):
        noted.append((q, flat(deps), fn, a, k, q))
        return len(noted) - 1

    def dma(q, deps, sem, out, in_):
        noted.append((q, flat(deps), eng[q].dma_start, (out, in_), {}, sem))
        return (sem, 16)

    calls = {"copy": g.vector.tensor_copy, "tt": g.vector.tensor_tensor, "ts": g.vector.tensor_scalar,
             "scan": g.vector.tensor_tensor_scan, "tr": g.vector.transpose, "set": g.vector.memset, "q": g.vector.quantize_mx}
    V = lambda deps, name, *a, **k: run("vq", deps, calls[name], *a, **k)
    S = lambda deps, *a, **k: run("sq", deps, g.scalar.activation, *a, **k)
    G = lambda deps, fn, *a, **k: run("gq", deps, fn, *a, **k)
    MM = lambda deps, out, l, r, a, b: run("tq", deps, g.tensor.matmul_mx, out, l[0], l[1], r[0], r[1], a, b)
    used = [[] for _ in range(8)]
    PS = [T["ps%d" % i] for i in range(8)]

    def C(n, a=0, b=None, st=1):
        buf, s, w = VIEW[n]
        b = w if b is None else b
        return T[buf][:, s + a:s + b] if st == 1 else T[buf][:, s + a:s + b:st]

    def back(n, a, b):
        buf, s, w = VIEW[n]
        return T[buf][:, s + b - 1:s + a - 1:-1]

    def qp(n, a=0, b=None):
        c, s = T[n + "c"], T[n + "s"]
        b = c.shape[1] if b is None else b
        return c[:, a:b], s[:, a:b]

    def quant(deps, n, a, b, tile):
        c, s = qp(n, a, b)
        return V(deps, "q", c, s, tile)

    def pickq(deps, to, frm, o):
        return [V(deps, "copy", w4(to[0]), w4(frm[0]).indirect(o)), S(deps, to[1], frm[1].indirect(o), AF.Copy)]

    lx = dma("sync", [], "ldx", T.xin[:, 0:512], T.x[:])
    lrt = dma("sq", [], "ldrt", T.rtin[:, 0:32], T.rt[:, 0:32])
    lgr = dma("sync", [], "ldgr", T.grin[:, 0:512], T.gr[:])
    lpr = dma("sq", [], "ldpr", T.prin[:], T.pr[:, 0:32])
    lw = dma("sync", [], "ldw", T.win[:], T.w[:])
    lu = dma("sync", [], "ldu", T.ubin[:], T.ub[:])
    lv = dma("sync", [], "ldv", T.vin[:], T.v[:])

    flags = dict(allow_small_or_imprecise_dtypes=True)
    iota = lambda n, pat, base, cm: G([], g.iota, C(n), pat, base, cm, **flags)
    gip = G([], g.iota, C("ip"), [[0, 8]], 0, 1)
    gic = G([], g.iota, C("ic"), [[16, 8]], 0, 0)
    gkr = iota("kr", [[1, 40]], 0, 0)
    gon = iota("ones", [[0, 128]], 1, 0)
    gid = G([gon], g.affine_select, C("idn"), C("ones"), [[-1, 128]], OP.is_equal, 0.0, 0, 1)
    gci = G([], g.iota, C("ci"), [[0, 2], [1, 4]], 0, 0)
    gcs = iota("cse", [[0, 4], [64, 8]], -1, 0)
    gva = iota("vals", [[1, 128]], 0, 0)
    gi2 = iota("its", [[0, 8], [-2, 16]], 46, 0)
    vz = V([], "set", T.zt[:], 0.0)
    fill = lambda out: S([vz], out, T.zt[:, 0:out.shape[1]], AF.Copy)
    frt = fill(T.rtin[:, 32:512])
    ra = V([gip], "ts", C("ra"), C("ip"), 15, None, OP.bitwise_and)
    vr1 = V([], "set", C("rs"), BIG)
    jj = V([ra, gic], "tt", C("jj"), C("ra"), C("ic"), OP.add)
    vr2 = V([vr1], "set", C("rs", 0, 32, 8), -BIG)
    eb = V([jj], "ts", C("eb"), C("jj"), 2, 7, OP.logical_shift_right, OP.bitwise_and)
    kq = V([gip], "ts", C("kq"), C("ip"), 3, None, OP.bitwise_and)
    l1 = V([eb], "copy", C("lb"), C("eb"))
    kt = V([kq], "ts", C("kthr"), C("kq"), 32, None, OP.mult)
    vxt = V([], "set", T.xin[:, 512:4 * OWN], 0.0)
    vgt = V([], "set", T.grin[:, 512:4 * OWN], 0.0)
    vs1, vs2, vs3 = [V([], "set", v, 0.0) for v in (T.st[:, 28:168:132], C("pfa", 0, 80, 72), C("fb", 3, 128, 4))]
    vcb = V([], "set", T.cb[:, 0:65 * NV:65], 512.0)
    ta = V([jj], "ts", C("ta"), C("jj"), 43, None, OP.mult)
    ua = V([jj], "ts", C("ua"), C("jj"), 86, None, OP.mult)
    tb = V([ta], "ts", C("tb"), C("ta"), 8, None, OP.logical_shift_right)
    ub = V([ua], "ts", C("ub"), C("ua"), 8, None, OP.logical_shift_right)
    tc = V([tb], "ts", C("tc"), C("tb"), -60, None, OP.mult)
    uc = V([ub], "ts", C("uc"), C("ub"), 29, None, OP.mult)
    td = V([tc, jj], "tt", C("td"), C("tc"), C("jj"), OP.add)
    ud = V([td, uc], "tt", C("ud"), C("td"), C("uc"), OP.add)
    l2 = V([ud], "copy", C("lc"), C("ud"))
    kk = S([kt, gkr], C("kk"), C("kr"), AF.Identity, bias=C("kthr", 0, 1))
    fe = [fill(T.e4[:, 512 * i:512 * i + 512]) for i in range(4)]
    ie = [S([gid, fe[i]], T.e4[:, 512 * i + i:512 * i + 512:4], C("idn"), AF.Copy) for i in range(4)]

    qrt = quant([lrt, frt], "rt", 0, 128, T.rtin[:])
    prt = pickq([qrt, l1], qp("rp"), qp("rt"), C("lb"))
    qx = quant([lx, vxt], "own", 0, OWN, T.xin[:])
    ms = MM([prt, qx], PS[0][:, 0:128], qp("rp"), qp("own", 0, 128), True, True)
    tr = V([ms], "tr", T.st[:, 32:160], PS[0][:, 0:128])
    used[0] = [tr]
    X, before, behind = T.st[:, 32:160:4], T.st[:, 28:156:4], T.st[:, 160:32:-4]
    pf = V([tr, vr2, vs1], "scan", C("pfa", 1, 33), before, C("rs"), 0.0, OP.max, OP.min)
    pr = V([tr, vr2, vs1], "scan", back("pra", 0, 32), behind, C("rs"), 0.0, OP.max, OP.min)
    qf = V([pf, vs2], "scan", C("pfb"), before, C("pfa", 0, 32), 0.0, OP.max, OP.min)
    qr = V([pr, vs2], "scan", back("prb", 0, 32), behind, back("pra", 1, 33), 0.0, OP.max, OP.min)
    c2 = V([pr], "tt", C("nra"), C("pra", 0, 32), X, OP.is_le)
    c1 = V([pf], "tt", C("nla"), C("pfa", 1, 33), X, OP.is_ge)
    c4 = V([qf], "tt", C("nlb"), C("pfb"), X, OP.is_ge)
    c3 = V([qr], "tt", C("nrb"), C("prb"), X, OP.is_le)
    m1 = V([c4, c2], "tt", C("nm"), C("nlb"), C("nra"), OP.is_ge)
    n2 = V([c3, c2], "tt", C("nr"), C("nra"), C("nrb"), OP.max)
    n1 = V([m1, c1], "tt", C("nl"), C("nla"), C("nm"), OP.min)
    fb = [V([n1, n2], "tt", C("fb", c, 128, 4), C("nr"), C("nl"), OP.is_gt) for c in range(3)]
    ft = V([fb, vs3], "tr", C("ft"), C("fb"))
    cum = V([ft, vz], "scan", C("cum"), C("ft"), T.zt[:, 0:128], 0.0, OP.add, OP.add)
    up = V([cum], "tt", back("up", 0, 64), C("cum", 0, 128, 2), C("cum", 1, 128, 2), OP.add)
    sa = [S([up, kk], T.jk[:, 64 * r:64 * r + 64], C("up"), AF.Sign, bias=C("kk", 2 * r + 1, 2 * r + 2), scale=-1.0, accum_out=C("xd", r, r + 1)) for r in range(NS)]
    d2 = S([sa], C("xd", 16, 16 + NS), C("xd", 0, NS), AF.Copy)
    cm = [V([up, kk], "ts", T.cb[:, 65 * r + 1:65 * r + 65], C("up"), C("kk", 2 * (NS + r) + 2, 2 * (NS + r) + 3), -2.0, OP.subtract, OP.max) for r in range(NV)]
    sn = V([cm, vcb, vz], "scan", T.cn[:, 0:65 * NV], T.cb[:, 0:65 * NV], T.zt[:, 0:65 * NV], 0.0, OP.add, OP.min)
    qg = quant([lgr, vgt], "own", OWN, 2 * OWN, T.grin[:])
    d1 = [V([sn], "ts", C("xd", h + NS, h + 16), T.cn[:, 64:65 * NV:65], -1.0, -64.0, OP.mult, OP.add) for h in (0, 16)]
    xo = V([d1, d2], "tr", C("xo"), C("xd"))
    xp = [V([xo], "ts", C("xp", 32 * u, 32 * u + 32), C("xo"), 64.0 + OWN * u, None, OP.add) for u in range(2)]
    of = V([xp, l2], "copy", T.off[:], C("xp").indirect(C("lc", 0, 3)))

    def runs(es):
        l = []
        for e in sorted(es):
            if l and l[-1][1] == e:
                l[-1][1] = e + 1
            else:
                l.append([e, e + 1])
        return [(qp("pk", 96 * lo, 96 * hi), T.off[:, 6 * lo:6 * hi]) for lo, hi in sorted(l, key=lambda r: r[0] - r[1])]
    ready, (oc, osc) = [of, qx, qg], qp("own")
    scales_s = lambda r: S(ready, r[0][1], osc.indirect(r[1]), AF.Copy)
    scales_v = lambda r: V(ready, "copy", r[0][1], osc.indirect(r[1]))
    codes = lambda r: V(ready, "copy", w4(r[0][0]), w4(oc).indirect(r[1]))
    rc, rn = runs(cross), runs(near)
    psc = [scales_s(rc[0]), scales_v(rc[1])]
    nsc = [scales_s(rn[0]), (scales_v if FW == "c" else scales_s)(rn[1])]
    pc = [codes(r) for r in rc]
    nc = [codes(r) for r in rn]
    o2 = V([xp], "copy", T.ofs[:, 0:3], C("xp", 32 + 4 * me, 35 + 4 * me))
    mine = [pickq(ready, qp("lxn", 0, 48), qp("own"), T.off[:, 6 * me:6 * me + 3]), pickq(ready + [o2], qp("lgn", 0, 48), qp("own"), T.ofs[:, 0:3])]

    offe = topo.engines(core, [cores[e] for e in near if not onchip(me, e)][0])
    one = [x for x in topo.engines(core, [cores[e] for e in near if onchip(me, e)][0]) if x not in offe]
    loc = [0]

    def fused(deps, trs):
        l = []
        for d, es, s, a, b in trs:
            rid, pid = topo.addr(d, core)
            l.append(RemoteDMATransfer(dst_ids=[DstId(rid=rid, pnc=pid)], dma_engine_mask=bits(es), remote_sem=T.sem[s], src=a, dst=b))
            loc[0] += len(es)
        noted.append(("gq", flat(deps), g.remote_dma_fused, (l,), dict(local_sem=T.sem.loc), None))

    hop, nhop, ka, kb = {}, {}, 0, 0
    for e in cross:
        h = road[(me, e)]
        if h in topo.cores_of(core):
            hop[e], ka = (h, one[ka:ka + 4]), ka + 4
        else:
            hop[e], kb = (h, offe[kb:kb + 4]), kb + 4
    kb = 0
    for e in near:
        if onchip(me, e):
            nhop[e] = one
        else:
            nhop[e], kb = offe[kb:kb + 4], kb + 4
    half = lambda l, i: l[len(l) // 2 * i:len(l) // 2 * (i + 1)]
    at = lambda e: 48 * seat(e).index(me)
    two = [(e, i, 96 * e + 48 * i, ("lxn", "lgn")[i]) for e in near for i in range(2)]
    ns_ = lambda es: [(cores[e], es(e, i), "nsc", T.pks[:, p:p + 48], T[b + "s"][:, at(e):at(e) + 48]) for e, i, p, b in two]
    nc_ = lambda es, ks: [(cores[e], es(e, i), ("nxo", "ngo")[i], by(T.pkc[:, p:p + 48]), by(T[b + "c"][:, at(e):at(e) + 48])) for e, i, p, b in two if i in ks]
    halves = lambda e, i: half(nhop[e], i)
    if FW == "c":
        ce = lambda e, i: hop[e][1][i:i + 1]
        ne = lambda e, i: nhop[e][2 + 4 * i:4 + 4 * i] if onchip(me, e) else nhop[e][2 + i:3 + i]
        fused([psc, nsc], [(hop[e][0], ce(e, i), "hsi", T.pks[:, 96 * e + 48 * i:96 * e + 48 * i + 48], T.hds[:, 48 * i:48 * i + 48]) for e in cross for i in range(2)] + ns_(ne))
        fused([pc, nc], [(hop[e][0], ce(e, i), "hci", by(T.pkc[:, 96 * e + 48 * i:96 * e + 48 * i + 48]), by(T.hdc[:, 48 * i:48 * i + 48])) for e in cross for i in range(2)]
              + nc_(ne, (0, 1)))
    else:
        fused(psc, [(*hop[e], "hsi", T.pks[:, 96 * e:96 * e + 96], T.hds[:]) for e in cross])
        fused(pc, [(*hop[e], "hci", by(T.pkc[:, 96 * e:96 * e + 96]), by(T.hdc[:])) for e in cross])
        fused(nsc, ns_(halves))
        if FW == "b":
            fused(nc, nc_(halves, (0, 1)))
        else:
            for k in range(2):
                fused(nc, nc_(lambda e, i: nhop[e], (k,)))
    n_s, n_c = {"a": (16, 16), "b": (16, 8), "c": (8, 4)}[FW]

    o, p = VIEW["wm"][1], VIEW["ones"][1]
    gwm = V([gid], "set", C("ones", 48, 49), 0.0)
    for a in range(0, 128, 32):
        gwm = G([gwm], g.affine_select, T.kb[a:a + 32, o:o + 98], T.kb[a:a + 32, p:p + 98], [[32, 2], [-1, 49]], OP.not_equal, -1.0, 0, 1)
    QUARTERS = range(4)
    piece = lambda d, n, buf, i: quant(d, n, 128 * i, 128 * i + 128, buf[:, 512 * i:512 * i + 512])
    qw = [piece([lw], "ww", T.win, i) for i in QUARTERS]
    qe = [piece([ie[i]], "ee", T.e4, i) for i in QUARTERS]
    qu = [piece([lu], "uu", T.ubin, i) for i in QUARTERS]
    vset = {b: V([], "set", T["f" + b][:, 48:64], -1.0) for b in "nc"}
    qpr = quant([S([lpr, vz], T.prt[:, t:512:4], T.zt[:, 0:128], AF.Identity, bias=T.prin[:, t:t + 1]) for t in QUARTERS], "pq", 0, 128, T.prt[:])
    fk = fill(T.kt[:])
    foh = {b: fill(T["big" + b][:, 2304:2816]) for b in "cn"}
    vrs = S([vz], T.rsw[:], T.zt[:, 0:512], AF.Identity, bias=128.0)
    k1 = V([gip], "ts", C("ka"), C("ip"), 31, None, OP.bitwise_and)
    k3 = V([gip], "ts", C("qi"), C("ip"), 5, None, OP.logical_shift_right)
    hi = V([k1, ra], "tt", C("kh"), C("ka"), C("ra"), OP.subtract)
    lo = V([ra], "copy", C("klo"), C("ra"))
    mk = V([k3, gci], "tt", C("mk"), C("qi"), C("ci"), OP.is_equal)
    veq = {b: V([], "set", T["big" + b][:, 2864:2865], 0.0) for b in "nc"}
    ix = V([k3], "ts", C("kix"), C("qi"), 48.0, 32.0, OP.mult, OP.add)
    hx = V([hi, k3], "ts", C("khx"), C("qi"), 48.0, C("kh", 0, 1), OP.mult, OP.add)
    kl = [V([mk, d, fk], "ts", T.kt[:, c:c + 4 * w - c % 2:4], C("mk", 0, w), s, None, OP.mult)
          for c, w, d, s in ((0, 8, lo, C("klo", 0, 1)), (1, 8, lo, C("klo", 0, 1)), (32, 4, hx, C("khx", 0, 1)), (33, 4, ix, C("kix", 0, 1)),
                             (48, 4, hi, C("kh", 0, 1)), (49, 4, mk, 32.0))]
    qk = quant([kl, V([fk], "set", T.kt[0:1, 50:66:4], 64.0 * me)], "kk", 0, 136, T.kt[:])
    ones = {b: V([foh[b]], "set", T["big" + b][0:1, 2306:2816:4], 1.0) for b in "cn"}
    ct = V([cum], "tr", C("ctr"), C("cum"))
    va = V([ct], "ts", C("va"), C("ctr", 0, 128, 4), 49.0, None, OP.min)
    ia = V([c1, c2], "tt", C("iab", 0, 32), C("nra"), C("nla"), OP.is_gt)
    vb = V([va, gcs], "tt", C("vb"), C("va"), C("cse"), OP.add)
    ib = V([ia, fb], "tt", C("iab", 32, 64), C("fb", 0, 128, 4), C("iab", 0, 32), OP.subtract)
    ma = V([vb, ia], "tt", C("vab", 0, 32), C("vb"), C("iab", 0, 32), OP.mult)
    mb = V([vb, ib], "tt", C("vab", 32, 64), C("vb"), C("iab", 32, 64), OP.mult)
    h1 = V([ma, mb], "tt", C("vac"), C("vab", 0, 64, 2), C("vab", 1, 64, 2), OP.add)
    h2 = V([h1], "tt", C("vad"), C("vac", 0, 32, 2), C("vac", 1, 32, 2), OP.add)
    h3 = V([h2], "tt", C("vae"), C("vad", 0, 16, 2), C("vad", 1, 16, 2), OP.add)
    og = [V([h3], "copy", T.offg[:, u:16:2], C("vae")) for u in range(2)]
    qv = quant([lv], "vv", 0, 128, T.vin[:])
    qzc = quant([vz], "cam", 128, 256, T.zt[:, 0:512])
    vcf = V([], "set", C("cf"), 0.0)

    R, free = {}, list(range(1, 8)) + [0]
    n_h = 16 if HOP == 2 else 32
    come = {"nf": [mine[0], ("nsc", n_s), ("nxo", n_c)], "nd": [mine[1], ("nsc", n_s), ("ngo", n_c)], "cf": [("csc", 32), ("cxo", n_h)], "cd": [("csc", 32), ("cgo", n_h)]}

    def product(key, deps, l, r):
        o = free.pop(0)
        R[key] = MM([deps, used[o]], PS[o][:, 0:192], l, r, True, True), o

    def give(key, deps):
        o = R[key][1]
        used[o] = deps
        free.append(o)

    def forward(b, i):
        product((b, "f", i), [come[b + "f"], qw[i]], qp("ww", 128 * i, 128 * i + 128), qp("lx" + b))

    def unpack(b, i):
        product((b, "d", i), [come[b + "d"], qe[i]], qp("ee", 128 * i, 128 * i + 128), qp("lg" + b))

    def mask_s(b, i):
        B, (f, o) = T["big" + b], R[b, "f", i]
        m = B[:, 2944 + 192 * i:3136 + 192 * i]
        s = S([f], m, PS[o][:, 0:192], AF.Sign)
        give((b, "f", i), [s])
        R[b, "k", i] = S([s], B[:, 192 * i:192 * i + 192], m, AF.Relu)

    def mask_v(b, i):
        f, o = R[b, "f", i]
        R[b, "k", i] = V([f], "ts", T["big" + b][:, 192 * i:192 * i + 192], PS[o][:, 0:192], 0.0, None, OP.is_gt)
        give((b, "f", i), [R[b, "k", i]])

    def masked(b, i):
        B, (d, o) = T["big" + b], R[b, "d", i]
        R[b, "m", i] = V([R[b, "k", i], d], "tt", B[:, 768 + i:1536:4], PS[o][:, 0:192], B[:, 192 * i:192 * i + 192], OP.mult)
        give((b, "d", i), [R[b, "m", i]])

    def quant_m(b):
        R[b, "qm"] = quant([R[b, "m", i] for i in QUARTERS], "mm" + b, 0, 192, T["big" + b][:, 768:1536])

    def strengths(b):
        product((b, "st"), [R[b, "qm"], qpr], qp("pq"), qp("mm" + b))

    def before_dx(b, i):
        product((b, "u", i), [R[b, "qm"], qu[i]], qp("uu", 128 * i, 128 * i + 128), qp("mm" + b))

    def sizes(b):
        F, (st, o) = T["f" + b], R[b, "st"]
        R[b, "ab"] = [S([st], F[32 * a:32 * a + 32, 0:48], PS[o][32 * a:32 * a + 32, 48 * a:48 * a + 48], AF.Abs) for a in range(4)]
        give((b, "st"), R[b, "ab"])

    def turn(b):
        F = T["f" + b]
        R[b, "tn"] = V([R[b, "ab"], vset[b]], "tr", F[:, 64:128], F[:, 0:64])

    def scaled(b, i, on_scalar):
        B, (u, o) = T["big" + b], R[b, "u", i]
        out, in_ = B[:, 1536 + i:2304:4], PS[o][:, 0:192]
        R[b, "x", i] = S([u], out, in_, AF.Copy, scale=0.0625) if on_scalar else V([u], "ts", out, in_, 0.0625, None, OP.mult)
        give((b, "u", i), [R[b, "x", i]])

    def signs(b):
        F = T["f" + b]
        R[b, "sg"] = [S([R[b, "tn"], R[b, "ab"]], F[:, 256 + 48 * t:304 + 48 * t], F[:, 0:48], AF.Sign, bias=F[:, 64 + 32 * t:65 + 32 * t], scale=-1.0,
                        accum_out=F[:, 160 + t:161 + t]) for t in range(2)]

    def equals(b):
        B, F = T["big" + b], T["f" + b]
        eq = [V([R[b, "tn"]], "ts", B[:, 2816 + 49 * t:2864 + 49 * t], F[:, 0:48], F[:, 64 + 32 * t:65 + 32 * t], None, OP.is_equal) for t in range(2)]
        R[b, "er"] = V([eq, gwm, veq[b]], "scan", F[:, 352:449], B[:, 2816:2913], C("wm", 0, 97), 0.0, OP.add, OP.mult)

    def one_hot(b):
        B, F = T["big" + b], T["f" + b]
        oh = [V([R[b, "er"], R[b, "sg"][t], gi2, foh[b]], "ts", B[:, 2304 + t:2816:4], C("its"), F[:, 160 + t:161 + t], F[:, 399 + 49 * t:400 + 49 * t],
                OP.subtract, OP.is_equal) for t in range(2)]
        R[b, "oh"] = quant([oh, ones[b]], "oh" + b, 0, 128, B[:, 2304:2816])

    def lists(b):
        o = free.pop(0)
        MM([R[b, "oh"], qk, used[o]], PS[o][:, 0:128], qp("oh" + b), qp("kk", 0, 128), True, False)
        R[b, "l"] = MM([], PS[o][:, 0:128], qp("oh" + b), qp("kk", 8, 136), False, True), o

    def quant_dx(b):
        R[b, "qd"] = quant([R[b, "x", i] for i in QUARTERS], "dd" + b, 0, 192, T["big" + b][:, 1536:2304])

    def entries(b):
        l, o = R[b, "l"]
        R[b, "ll"] = V([l], "copy", T["ll" + b][:], PS[o][:, 0:8])
        give((b, "l"), [R[b, "ll"]])

    def answers(b):
        R[b, "rc"], R[b, "rs"] = pickq([R[b, "qd"], R[b, "ll"]], qp("rr" + b), qp("dd" + b), T["ll" + b][:, 0:4])

    def own_answers(b):
        R["own"] = pickq([R[b, "qd"], R[b, "ll"]], qp("cam", 112, 128), qp("dd" + b), T["ll" + b][:, 0:1])

    def send(b):
        rr, rs, ll = T["rr" + b + "c"], T["rr" + b + "s"], T["ll" + b]
        k = lambda e: near_of(e).index(me)
        n = 2 if PAIRS else 1
        for name, hsem, nsem, src, hland, land in (
                ("ll", "hli", "rln", lambda i, n: ll[:, 4 + i:4 + i + n], T.hrl[:, 0:n], lambda e: T.lland[:, 4 + k(e):5 + k(e)]),
                ("rc", "hri", "rcn", lambda i, n: by(rr[:, 16 * i:16 * (i + n)]), by(T.hrc[:, 0:16 * n]), lambda e: by(T.camc[:, 64 + 16 * k(e):80 + 16 * k(e)])),
                ("rs", "hrsi", "rsn", lambda i, n: rs[:, 16 * i:16 * (i + n)], T.hrs[:, 0:16 * n], lambda e: T.cams[:, 64 + 16 * k(e):80 + 16 * k(e)])):
            if b == "n":
                fused([R[b, name]], [(cores[e], nhop[e], nsem, src(seat(me).index(e), 1), land(e)) for e in near])
            elif PAIRS:
                here = [e for e in cross if hop[e][0] in topo.cores_of(core)]
                fused([R[b, name]], [(hop[e][0], (offe, one)[i], hsem, src(cross.index(e) // 2 * 2, 2), hland) for i, e in enumerate(here)])
            else:
                fused([R[b, name]], [(*hop[e], hsem, src(i, 1), hland) for i, e in enumerate(cross)])

    stage = {"f": forward, "d": unpack, "s": mask_s, "k": mask_v, "m": masked, "q": quant_m, "t": strengths, "u": before_dx, "a": sizes, "n": turn,
             "x": lambda b, i: scaled(b, i, True), "y": lambda b, i: scaled(b, i, False), "g": signs, "e": equals, "o": one_hot, "l": lists,
             "z": quant_dx, "v": entries, "r": answers, "w": send, "O": own_answers}
    for s in PLAN.split():
        stage[s[1]](s[0], *[int(i) for i in s[2:]])
    (own, owns), lln, n_r = R["own"], R["n", "ll"], 16 if PAIRS else 32

    sc1 = V([vrs, lln, gva], "copy", T.rsw[:].indirect(T.lln[:, 4:5]), C("vals", 112, 128))
    sc2 = V([sc1, ("rlc", n_r)], "copy", T.rsw[:].indirect(T.lland[:, 0:4]), C("vals", 0, 64))
    sc3 = V([sc2, ("rln", 16)], "copy", T.rsw[:].indirect(T.lland[:, 4:7]), C("vals", 64, 112))
    part = lambda h, w: slice(w * h, w * h + w)
    ga = V([sc3, og], "copy", T.gg[:, 0:128], T.rsw[:].indirect(T.offg[:, 0:8]))
    gb = S([sc3, og], T.gg[:, 128:256], T.rsw[:].indirect(T.offg[:, 8:16]), AF.Copy)
    gt = [V([d], "tr", T.gt[:, part(h, 128)], T.gg[:, part(h, 128)]) for h, d in enumerate((ga, gb))]
    fo = V([gt], "copy", T.fo[:], T.gt[:, 0:256:16])
    cc, cs = [("rcn", 16), ("rcc", n_r), qzc, own, fo], [("rsn", 16), ("rsc", n_r), qzc, owns, fo]
    zc = [V(cc, "copy", w4(T.zpc[:, part(h, 128)]), w4(T.camc[:]).indirect(T.fo[:, part(h, 8)])) for h in range(2)]
    zs = [S(cs, T.zps[:, 0:128], T.cams[:].indirect(T.fo[:, 0:8]), AF.Copy), V(cs, "copy", T.zps[:, 128:256], T.cams[:].indirect(T.fo[:, 8:16]))]
    f1 = V([gt], "ts", C("cfa"), T.gt[:, 0:128:16], 127.5, None, OP.is_lt)
    f2 = V([gt], "ts", C("cfb"), T.gt[:, 128:256:16], 127.5, 2.0, OP.is_lt, OP.mult)
    f3 = V([f1, f2, vcf], "tt", C("cf", 0, 8), C("cfa"), C("cfb"), OP.add)
    f4 = V([f3], "tr", C("cft"), C("cf"))
    hf, o = VIEW["cft"][:2]
    dma("sync", [f4], "outs", T.ct[:], T[hf][0:8, o:o + 16])
    zt, home = [], free[:5]
    for i in QUARTERS:
        for h in range(2):
            b = home[i]
            o = PS[b][:, 0:128]
            t = MM([zc[h], zs[h], qe[i], used[b]], o, qp("ee", 128 * i, 128 * i + 128), qp("zp", 128 * h, 128 * h + 128), h == 0, h == 1)
        zt.append(V([t], "copy", T.zz[:, i:512:4], o) if i % 2 else S([t], T.zz[:, i:512:4], o, AF.Copy))
    zq = quant(zt, "zq", 0, 128, T.zz[:])
    dma("sync", [zq], "outs", T.oc[:], by(T.zqc[:]))
    for k in range(4):
        dma("sync" if k < 2 else "sq", [zq], "outs" if k < 2 else "outs2", T.osc[4 * k:4 * k + 4, :], T.zqs[32 * k:32 * k + 4, :])
    ym = MM([zq, qv, used[home[4]]], PS[home[4]][:, 0:128], qp("vv"), qp("zq"), True, True)
    yc = V([ym], "copy", T.yo[:], PS[home[4]][:, 0:128])
    dma("sq", [yc], "outs2", T.y[:], T.yo[:])

    cnt, seen, done = {q: 0 for q in eng}, {q: {} for q in eng}, {}

    def wait(q, deps):
        best = {}
        for s, n in deps:
            best[s] = max(best.get(s, 0), n)
        for s, n in best.items():
            if seen[q].get(s, 0) < n:
                eng[q].wait_ge(T.sem[s], n)
                seen[q][s] = n

    for i in [int(t) for t in ORDER.split()] or range(len(noted)):
        q, deps, fn, a, k, sem = noted[i]
        wait(q, [done[d] if isinstance(d, int) else d for d in deps])
        call = fn(*a, **k)
        if sem == q:
            call.then_inc(T.sem[q], 1)
            cnt[q] += 1
            done[i] = (q, cnt[q])
        elif sem:
            call.then_inc(T.sem[sem], 16)
    wait("gq", [(s, cnt[s]) for s in ("vq", "sq", "tq", "gq")] + [lx, lrt, lgr, lw, lpr, lu, lv, ("outs", 64), ("outs2", 48), ("loc", loc[0])])
